import numpy as np, ml_dtypes
CORES = [3,7,11,15,131,135,139,143]
N = 8
BF = ml_dtypes.bfloat16
W, P, R, M0, M, S, RO, TH = 2048, 128, 128, 384, 896, 3, 2, 620
def even(rng, *shape):
    return rng.integers(0, W - 1, shape)
def uneven(rng, *shape):
    return np.minimum(np.exp2(11 * rng.random(shape)).astype(np.int64) - 1, W - 2)
def edgy(rng, *shape):
    return (rng.random(shape) < 0.4) * (W - 2)
def across(t):
    y = t ^ (W // 2)
    return np.where(y == W - 1, W - 2, y)
def look(rng):
    x = rng.integers(0, 256, (16, W)); h = W // 2; m = rng.choice(np.array([0, 8, 40, 90, 120]), h)
    x[:, h:] = np.clip(x[:, :h] + rng.integers(-m, m + 1, (16, h)), 0, 255)
    return x
def rough(rng):
    return np.minimum((np.exp2(8 * rng.random((1, W))) * rng.random((16, W))).astype(np.int64), 255)
def grow(rng, tok, stem, slots, keep=0):
    k = np.arange(16)[:, None]; o = R + keep + rng.permutation(M0 - R - 2 * keep); h = len(o) // 2
    L = np.full((16, M0), W - 1); ch = np.zeros((16, M0), np.int64); F = tok(rng, 16, M0); e = np.zeros(M0, np.int64)
    levels = [np.arange(R), o[:h], o[h:h + h // 2], o[h + h // 2:]]
    for z in range(3):
        up, dn = levels[z], levels[z + 1]; n = len(dn)
        x = rng.permutation(slots)[:n] if z == 0 else rng.permutation(16 * len(up))[:n]
        p, t = up[x >> 4], x & 15; T = tok(rng, 16, n)
        if z == 0:
            T = np.where(rng.random((16, n)) < 0.8, stem[:, x], T); T[0] = x
        s = e[p]; e[dn] = np.minimum(16, s + rng.choice(np.array([1, 1, 2, 3, 5, 8, 16]), n))
        y = (T & -16) + t; T = np.where(k == s, np.where(y == W - 1, W - 17, y), T)
        F[:, dn] = np.where(k < s, F[:, p], T)
        stray = (rng.random(n) < 0.125) & (rng.random((16, n)) < 0.5) & (k != e[dn])
        L[:, dn] = np.where((k >= s) & (k < e[dn]), T, np.where(stray, tok(rng, 16, n), W - 1)); ch[t, p] = dn
        if z == 0: L[0, dn] = np.where(rng.random(n) < 0.1, tok(rng, n), L[0, dn])
    return L, ch, F
def ask(rng, tok, F):
    k = np.arange(16)[:, None]; q = F[:, rng.integers(R, M0, P)]; z = rng.integers(1, 17, P); near = q ^ (W // 2)
    q = np.where((k > 0) & (rng.random((16, P)) < 0.3) & (near != W - 1), near, q)
    y = tok(rng, 16, P); y = np.where(rng.random((16, P)) < 0.5, (y & -16) + (q & 15), y); y = np.where(y == W - 1, W - 17, y)
    return np.where((k >= z) | (rng.random(P) < 0.125), y, q)
def draw(rng, tok, shape):
    h = (M0 - R) // 2; stem = [tok(rng, 16, W) for g in range(8)]; slots = [rng.permutation(W - 1)[:h + h // 4] for g in range(8)]; d = []
    for r in range(N):
        for g in range(8):
            L, ch, F = grow(rng, tok, stem[g], slots[g]); d.append([shape(rng), L, ch, ask(rng, tok, F)])
    return d
def apart(rng):
    return 16 * rng.permutation(R)[:P] + rng.integers(0, 15, P)
def pack(d):
    a = [np.stack([x[z] for x in d]).reshape(N, 128, -1) for z in range(4)]
    return {"desc": a[0].astype(np.float32).astype(BF), "edge": a[1].astype(np.int32), "child": a[2].astype(np.int32), "req": a[3].astype(np.int32)}
def setup_inputs(rng):
    return pack(draw(rng, even, look))
def setup_inputs_spread(rng):
    return pack(draw(rng, uneven, rough))
def setup_inputs_ends(rng):
    k = np.arange(16)[:, None]; h = (M0 - R) // 2; d = []
    stem = [edgy(rng, 16, W) for g in range(8)]; slots = [2 + rng.permutation(W - 18)[:h + h // 4] for g in range(8)]
    for r in range(N):
        for g in range(8):
            L, ch, F = grow(rng, edgy, stem[g], slots[g], 1)
            x = rng.integers(0, 2, (16, W)) * 255; x[:, 0] = 0; x[:, W - 2] = 255; x[:8, W // 2] = 0; x[8:, W // 2] = 255
            q = np.where(k >= rng.integers(1, 17, P), edgy(rng, 16, P), F[:, rng.integers(R + 1, M0 - 1, P)])
            ch[0, 0] = R; ch[1, 0] = 1; ch[14, R - 1] = M0 - 1
            L[:, R] = 0; L[15, R] = W // 2; L[:, M0 - 1] = 0; L[0, M0 - 1] = W - 2
            q[:, 0] = 0; q[15, 0] = W - 2; q[0, 1] = 1
            q[:, P - 1] = 0; q[0, P - 1] = W - 2; q[15, P - 1] = W - 2
            if g % 2: q[14, P - 1] = W - 2
            d.append([x, L, ch, q])
    return pack(d)
def setup_inputs_corners(rng):
    k = np.arange(16)[:, None]; i = np.arange(P); d = draw(rng, even, look)
    for j in range(8 * N):
        x, L, ch, q = d[j]; z = j % 11; q0 = apart(rng)
        if z in (2, 3, 4, 6, 8, 9, 10):
            ch[:] = 0; L[:] = W - 1
        if z in (9, 10):
            x = np.concatenate([rng.integers(0, 100, (16, W // 2)), rng.integers(156, 256, (16, W // 2))], axis=1)
        if z == 0:
            ch[:] = 0; q[0] = rng.choice(np.array([0, 1, 15, 16, W - 17, W - 2]), P)
            L[:, 0] = np.where(k < 8, q[:, :1], W - 1)[:, 0]
        if z == 1:
            y = int(rng.choice(np.flatnonzero(ch[:, :R].T.reshape(-1)))); e = L[:, ch[y & 15, y >> 4]][:, None]
            q = np.where((rng.random(P) < 0.5) & (k > 0) & (e < W - 1), e, q); q[0] = y
        if z in (2, 3):
            q = even(rng, 16, P); q[0] = q0; u = R + i if z == 2 else q0 >> 4; ch[q0 & 15, q0 >> 4] = u; m = rng.integers(0, 5, P)
            e = np.where(((m == 1) & (k == 15)) | ((m == 2) & (k == 0)) | ((m == 3) & (k == 1)), even(rng, 16, P), q)
            L[:, u] = np.where((m == 4) & (k >= (8 if z == 2 else np.maximum(rng.integers(-5, 16, P), 0))), W - 1, e)
        if z == 4:
            nc = (M0 - R) // 4; T = even(rng, 16, nc); T[0] = rng.permutation(W - 1)[:nc]
            for m in range(4):
                u = R + 4 * np.arange(nc) + m; L[m, u] = T[m]; ch[T[m] & 15, T[0] >> 4 if m == 0 else u - 1] = u
            q = T[:, i % nc]
        if z == 5: L[:] = W - 1
        if z == 6:
            q = even(rng, 16, P); q[0] = q0; w = q0 >> 4; a = np.flatnonzero(w % 2 == 0); ch[q0[a] & 15, w[a]] = w[a] + 1
            L[:, w[a] + 1] = np.where(k < rng.integers(1, 16, len(a)), q[:, a], even(rng, 16, len(a))); q[0] = np.where(w % 4 == 3, q0 - 32, q0)
        if z == 7: q[1:] = rng.choice(np.array([0, 1, W - 3, W - 2]), (15, 1))
        if z == 8:
            nb = P // N; nc = min((M0 - R) // 17, nb); a = rng.permutation(nb)[:nc]; o = nb + rng.permutation(P - nb)[:nc]
            m = rng.integers(2, 16, nc); p = rng.integers(1, m); u = R + 17 * np.arange(nc)
            q = even(rng, 16, P); q[0] = q0; q[:, o] = np.where(k < p, q[:, a], q[:, o]); T = q[:, a]
            h = ((T[1:] * T[:-1]) >> 5) & (W - 1); h = np.concatenate([T[:1], np.where(h == W - 1, 0, h)])
            ch[T[0] & 15, T[0] >> 4] = u; L[:, u] = np.where(k < m, T, W - 1)
            for t in range(16):
                e = m + rng.integers(0, 17 - m); ch[t, u] = u + 1 + t
                L[:, u + 1 + t] = np.where((k >= m) & (k < e), np.where(rng.random((16, nc)) < 0.1, even(rng, 16, nc), h), W - 1)
        if z == 9:
            q = even(rng, 16, P); q[0] = q0; nc = P // 16; n = np.arange(nc); c = R + n; m = rng.integers(1, 8, nc)
            s = np.sort(rng.permutation(np.flatnonzero(q0 > 15))[:9 * nc].reshape(9, nc), axis=0)
            u, o, uu, oo = [q0[s[t]] >> 4 for t in (0, 2, 8, 5)]; T = q[:, s[0]]; y = q[:, s[8]]
            q[:, s[1]] = np.where(k < m, T, np.where(k == m, np.where((T ^ 1) == W - 1, 0, T ^ 1), q[:, s[1]]))
            q[0, s[2:5]] = 16 * o + (rng.integers(0, 15, nc) + 5 * np.arange(3)[:, None]) % 15
            q[0, s[5:8]] = 16 * oo + (rng.integers(0, 15, nc) + 5 * np.arange(3)[:, None]) % 15
            ch[T[0] & 15, u] = c; ch[T[m, n] & 15, c] = o; ch[y[0] & 15, uu] = oo
            L[:, c] = np.where(k < m, T, W - 1); L[:, o] = np.where(k <= m, T, across(T))
            L[:, oo] = np.where(k < rng.integers(1, 16, nc), y, W - 1)
        if z == 10:
            q = even(rng, 16, P); q[0] = q0; ch[q0 & 15, q0 >> 4] = R + i; p = rng.integers(1, 16, P); y = across(q)
            y = np.where(rng.random(P) < 0.25, y, (y & -16) + rng.integers(0, 15, P))
            L[:, R + i] = np.where(k == p, y, q)
        d[j] = [x, L, ch, q]
    return pack(d)
def setup_inputs_ties(rng):
    k = np.arange(16)[:, None]; i = np.arange(P); h = 3 * P // 4; s = np.where(i < h, i, i - P // 2); d = []
    for j in range(8 * N):
        x = look(rng); b = 16 * rng.integers(0, R - 1, 16) + np.arange(16)
        A = rng.permutation(W - 1); A = A[~np.isin(A, b)][:P]; B = b[np.where(rng.random(P) < 0.25, A & 15, rng.integers(0, 16, P))]; p = rng.integers(1, 16, P)
        x[:, b] = rng.integers(100, 121, (16, 16)); y = TH + rng.integers(-1, 2, P); v = rng.integers(-20, 21, (8, P))
        D = (y >> 4) + (k < (y & 15)) + np.concatenate([v, -v])
        f1 = rng.integers(0, 16, P); f2 = f1 ^ (1 << rng.integers(0, 4, P)); w = np.where(y > TH, 257, 259); z = y - w; o = k - (k > f1) - (k > f2)
        D = np.where(rng.random(P) < 0.5, D, np.where(k == f1, w >> 1, np.where(k == f2, w - (w >> 1), z // 14 + (o < z % 14))))
        x[:, A] = x[:, B] + D * np.where(D > 100, 1, rng.choice(np.array([-1, 1]), (16, P)))
        T = even(rng, 16, P); T[0] = apart(rng); T = T[:, s]
        L = np.full((16, M0), W - 1); ch = np.zeros((16, M0), np.int64)
        L[:, R:R + h] = np.where(k == p, A, T)[:, :h]; ch[T[0] & 15, T[0] >> 4] = R + s
        d.append([x, L, ch, np.where(k == p, B, T)])
    return pack(d)
def check_inputs(d):
    bad = []
    for a, lo, hi in (("desc", 0, 255), ("edge", 0, W - 1), ("child", 0, M0 - 1), ("req", 0, W - 2)):
        x = np.asarray(d[a]).astype(np.float64)
        if not (np.min(x) >= lo and np.max(x) <= hi): bad.append("range of " + a)
        if np.any(x != np.floor(x)): bad.append("whole numbers in " + a)
    c = np.sort(np.asarray(d["child"]).reshape(N, 8, 16 * M0), axis=-1)
    if np.any((c[..., 1:] == c[..., :-1]) & (c[..., 1:] > 0)): bad.append("a node stands twice in child")
    return bad
def walk(X, L, C, Q, rnd):
    i = np.arange(P); k = np.arange(16)[:, None]; n = M0 + 2 * P * rnd + 2 * i
    v = Q[0] >> 4; a = np.zeros(P, np.int64); on = np.ones(P, bool)
    for step in range(S):
        low = np.full(M, P); np.minimum.at(low, v[on], i[on])
        act = on & (low[v] == i)
        t = Q[np.minimum(a, 15), i] & 15; c = C[t, v]; E = L[:, c]; none = E == W - 1
        dist = np.add.reduce(np.abs(X[:, E] - X[:, Q]), axis=0)
        b = np.min(np.where((k >= a) & none, k, 16), axis=0)
        l = np.min(np.where((k >= a) & (none | (dist > TH)), k, 16), axis=0)
        leaf = act & ((c == 0) | ((l == a) & (l < b)))
        down = act & (c > 0) & (l == b)
        cut = act & (c > 0) & (l > a) & (l < b) & (low[c] == P)
        j = np.flatnonzero(cut); lj = l[j]; cj = c[j]; ej = E[lj, j]; qj = Q[lj, j]
        f = np.unique(qj, return_index=True)[1]
        X[:, qj[f]] = (X[:, qj[f]] + X[:, ej[f]]) >> 1
        L[:, n[j]] = np.where(k >= lj, E[:, j], W - 1); C[:, n[j]] = C[:, cj]
        L[:, cj] = np.where(k < lj, E[:, j], W - 1); C[:, cj] = 0; C[ej & 15, cj] = n[j]
        two = (ej & 15) != (qj & 15); o = j[two]
        C[qj[two] & 15, cj[two]] = n[o] + 1; L[:, n[o] + 1] = np.where(k >= l[o], Q[:, o], W - 1)
        j = np.flatnonzero(leaf)
        L[:, n[j]] = np.where(k >= a[j], Q[:, j], W - 1); C[t[j], v[j]] = n[j]
        v = np.where(down, c, v); a = np.where(down, b, a); on = on & ~leaf & ~cut & (a < 16)
    return a
def reference(desc, edge, child, req):
    X = desc.astype(np.float32).astype(np.int64).reshape(N, 8, 16, W); Q = req.astype(np.int64).reshape(N, 8, 16, P)
    L = np.full((N, 8, 16, M), W - 1); L[..., :M0] = edge.reshape(N, 8, 16, M0)
    C = np.zeros((N, 8, 16, M), np.int64); C[..., :M0] = child.reshape(N, 8, 16, M0)
    k = np.arange(1, 16)[:, None]; B = P // N
    for rnd in range(RO):
        new = np.zeros_like(Q)
        for r in range(N):
            for g in range(8):
                q = Q[r, g]; a = walk(X[r, g], L[r, g], C[r, g], q, rnd)
                h = ((q[1:] * q[:-1]) >> 5) & (W - 1); h = np.where(h == W - 1, 0, h)
                q = np.concatenate([q[:1], np.where(k >= a, h, q[1:])])
                for e in range(N): new[(r + e) % N, g, :, e * B:(e + 1) * B] = q[:, e * B:(e + 1) * B]
        Q = new
    return {"yd": X.reshape(N, 128, W).astype(np.float32).astype(BF), "ye": L.reshape(N, 128, M).astype(np.float32), "yr": Q.reshape(N, 128, P).astype(np.float32)}

@@ -1,0 +1,660 @@
+from concourse.bass import DstId, RemoteDMATransfer
+from concourse.mybir import AluOpType as A, ActivationFunctionType as F
+
+S_, RO_ = 3, 2
+F32, BF, H16, I32, U16 = "float32", "bfloat16", "float16", "int32", "uint16"
+SCRATCH = {}
+
+
+PLACE = {}
+
+
+def _b(name, n, d, where="sbuf"):
+    pool = {F32: "poolf", U16: "poolu", I32: "pooli"}.get(d)
+    if name.startswith("QE"):
+        pool = "poolq"
+    elif n > 16 or where != "sbuf":
+        pool = None
+    if pool is None:
+        SCRATCH[name] = (where, [128, n], d)
+        PLACE[name] = (name, 0, n)
+    else:
+        at = SCRATCH[pool][1][1] if pool in SCRATCH else 0
+        SCRATCH[pool] = ("sbuf", [128, at + n + n % 2], d)
+        PLACE[name] = (pool, at, n)
+
+
+_b("X", 2192, BF); _b("L", 1152, F32); _b("C", 1152, F32); _b("BT", 2048, BF)
+_b("Ei", 384, I32); _b("Ci", 384, I32); _b("Qi", 128, I32); _b("xsave", 16, BF); _b("lsave", 4, F32)
+_b("IQ", 128, I32); _b("IP", 1, I32); _b("IC", 4, I32); _b("R4i", 256, I32); _b("Qb", 128, BF); _b("Q4b", 256, BF)
+_b("cols", 16, F32); _b("flip", 16, F32); _b("BO", 128, BF); _b("R", 128, BF); _b("CONV", 2048, BF)
+for _n in ("I", "TRI", "STRI", "SHD", "SHU", "D64", "Dm64", "DQ", "I64", "Im128", "IB", "ImB", "TRI64", "BO64", "BOm16", "BOm1",
+           "MSK", "B0", "ONES", "tmpc", "tmpd", "tmpe"):
+    _b(_n, 128, BF)
+_b("I32", 128, F32); _b("SEL", 8, BF); _b("SELB", 8, BF); _b("MASKN", 512, BF); _b("BAND", 240, BF); _b("Y0", 384, BF)
+_b("W8", 8, F32); _b("DUM", 16, F32); _b("DD", 16, F32); _b("DTOK", 8, F32); _b("N01", 512, F32)
+_b("Qi2", 128, I32); _b("QF", 128, F32); _b("Ql", 128, U16); _b("Q4i", 128, I32); _b("Q4m", 128, H16); _b("QMi", 128, I32)
+_b("QM", 128, H16); _b("uQ", 128, H16); _b("Q16", 128, H16); _b("HP", 128, I32); _b("HI", 128, I32); _b("HM", 128, F32)
+_b("HMQ", 128, F32); _b("HK", 128, F32); _b("SND", 128, F32); _b("LAND0", 128, F32); _b("LAND1", 128, F32)
+_b("vl", 8, U16); _b("cl", 8, U16); _b("VC", 16, F32); _b("OH", 128, F32); _b("P", 128, BF); _b("KGE", 128, BF)
+_b("M1", 128, H16); _b("mk", 128, H16); _b("mkq", 256, H16); _b("El", 128, U16); _b("XQ", 2048, BF); _b("DF", 2048, BF)
+_b("AB", 2048, BF); _b("VB", 128, BF); _b("VBo", 128, BF); _b("CB", 128, BF); _b("CV", 128, F32); _b("Cc", 128, F32)
+_b("uE", 128, F32); _b("EA", 1024, BF); _b("ED", 1024, BF); _b("ES", 1024, BF); _b("NA", 128, BF); _b("STD", 128, BF)
+_b("NN", 128, BF); _b("T1", 128, F32); _b("T2", 128, F32); _b("BUF", 512, H16)
+for _n in range(6):
+    _b("QE%d" % _n, 256, H16)
+_b("CMV", 8, F32); _b("DMC", 8, F32); _b("VCD", 16, F32); _b("WF", 16, F32); _b("x1", 8, F32); _b("x2", 8, F32)
+_b("x3", 8, F32); _b("x4", 8, F32); _b("w6", 16, F32); _b("y1", 8, F32); _b("l1", 16, F32); _b("l2", 16, F32)
+_b("lc", 16, U16); _b("qel", 16, U16); _b("QLF", 8, F32); _b("QB", 128, BF); _b("QBo", 128, BF)
+_b("XLg", 128, F32); _b("DS", 128, I32); _b("DH", 128, I32); _b("mk2", 128, H16); _b("d1", 8, F32); _b("d2", 8, F32)
+_b("didx", 8, U16); _b("X1", 128, H16); _b("X2", 128, F32); _b("X3", 128, H16); _b("X5", 128, F32)
+_b("RI", 256, I32); _b("RA", 256, I32); _b("OHc", 256, F32); _b("OHN", 256, F32); _b("YE", 896, F32)
+PS = ["pg0", "pg1", "pc", "pm", "pd", "py", "ps", "pw"]
+for _n in PS:
+    _b(_n, 512, F32, "psum")
+SEMAPHORES = ["sV", "sT", "sS", "sG", "loc", "arr0", "arr1"] + ["d%d" % _i for _i in range(12)]
+NDUM, NDUMP, TDUMP, BIG = 896, 1024, 2064, float(2 ** 17)
+
+
+def make(g, T):
+    eng = {"V": g.vector, "S": g.scalar, "T": g.tensor, "G": g, "Y": g.sync}
+    tick = {"V": 0, "S": 0, "T": 0, "G": 0}
+    known = {q: {} for q in eng}
+    snap, acc, final, ndma = {}, {}, {}, [0]
+
+    def ap(x):
+        if x[0] == "@":
+            return ap(x[1]).indirect(ap(x[2]))
+        t = T[x[0]]
+        st = x[3] if len(x) > 3 else 1
+        p0, p1 = (x[4], x[5]) if len(x) > 4 else (0, 128)
+        return t[p0:p1, x[1]:x[2]:st] if st != 1 else t[p0:p1, x[1]:x[2]]
+
+    def flat(xs):
+        out = []
+        for x in xs:
+            if x is None or isinstance(x, (int, float)):
+                continue
+            if x[0] == "@":
+                out += [x[1], x[2]]
+            else:
+                out.append(x)
+        return out
+
+    def wait(q, sem, val):
+        k = known[q]
+        if k.get(sem, 0) >= val:
+            return
+        eng[q].wait_ge(T.sem[sem], val)
+        k[sem] = val
+        for s, v in snap.get((sem, val), {}).items():
+            if k.get(s, 0) < v:
+                k[s] = v
+
+    def deps(q, reads, writes, sem, val, dma=False):
+        need = {}
+        for isw, xs in ((0, reads), (1, writes)):
+            for x in xs:
+                n, lo, hi = x[0], x[1], x[2]
+                ps = n in PS
+                for e in acc.get(n, []):
+                    elo, ehi, ew, eq, es, ev, ed = e
+                    if ps:
+                        if eq == q and (q == "T" or not (isw or ew) or ehi <= lo or hi <= elo):
+                            continue
+                    else:
+                        if ehi <= lo or hi <= elo or not (isw or ew):
+                            continue
+                    need[es] = max(need.get(es, 0), ev)
+        for s in sorted(need, key=lambda z: z == "s" + q):
+            wait(q, s, need[s])
+        for isw, xs in ((0, reads), (1, writes)):
+            for x in xs:
+                n, lo, hi = x[0], x[1], x[2]
+                full = len(x) < 5
+                l = acc.setdefault(n, [])
+                if isw and full and n not in PS and (len(x) < 4 or x[3] == 1):
+                    l[:] = [e for e in l if not (lo <= e[0] and e[1] <= hi)]
+                else:
+                    l[:] = [e for e in l if not (e[3] == q and not e[6] and not dma and e[0] == lo and e[1] == hi and e[2] == isw)]
+                l.append((lo, hi, isw, q, sem, val, dma))
+
+    def fin(q, ins):
+        sem = "s" + q
+        tick[q] += 1
+        snap[(sem, tick[q])] = dict(known[q])
+        final[sem] = tick[q]
+        ins.then_inc(T.sem[sem], 1)
+
+    def pre(q, reads, writes):
+        deps(q, flat(reads), flat(writes), "s" + q, tick[q] + 1)
+
+    def wr(out):
+        return ([out[1]], [out[2]]) if out[0] == "@" else ([out], [])
+
+    def tt(out, a, b, op):
+        w, r = wr(out)
+        pre("V", [a, b] + r, w)
+        fin("V", g.vector.tensor_tensor(ap(out), ap(a), ap(b), op))
+
+    def ts(out, a, s1, op0, s2=None, op1=None):
+        pre("V", [a, s1, s2], [out])
+        f = lambda s: ap(s) if isinstance(s, tuple) else s
+        if op1 is None:
+            fin("V", g.vector.tensor_scalar(ap(out), ap(a), f(s1), None, op0))
+        else:
+            fin("V", g.vector.tensor_scalar(ap(out), ap(a), f(s1), f(s2), op0, op1))
+
+    def cp(out, a):
+        w, r = wr(out)
+        pre("V", [a] + r, w)
+        fin("V", g.vector.tensor_copy(ap(out), ap(a)))
+
+    def ms(out, c):
+        pre("V", [], [out])
+        fin("V", g.vector.memset(ap(out), c))
+
+    def act(out, a, func, bias=0.0, scale=1.0):
+        pre("S", [a, scale], [out])
+        sc = ap(scale) if isinstance(scale, tuple) else scale
+        fin("S", g.scalar.activation(ap(out), ap(a), func, bias=bias, scale=sc))
+
+    def iota(out, pattern, base, cm, fl=False):
+        pre("G", [], [out])
+        if fl:
+            fin("G", g.iota(ap(out), pattern, base, cm, allow_small_or_imprecise_dtypes=True))
+        else:
+            fin("G", g.iota(ap(out), pattern, base, cm))
+
+    def sel(out, a, pattern, op, base, cm):
+        pre("G", [a], [out])
+        fin("G", g.affine_select(ap(out), ap(a), pattern, op, 0.0, base, cm))
+
+    def mm(lst):
+        pre("T", [x[1] for x in lst] + [x[2] for x in lst], [x[0] for x in lst])
+        for i, (o, l, r, st, sp) in enumerate(lst):
+            ins = g.tensor.matmul(ap(o), ap(l), ap(r), st, sp)
+            if i == len(lst) - 1:
+                fin("T", ins)
+        return tick["T"]
+
+    def dma(q, out, in_, r=(), w=()):
+        sem = "d%d" % ndma[0]
+        ndma[0] += 1
+        deps(q, list(r), list(w), sem, 16, True)
+        snap[(sem, 16)] = dict(known[q])
+        final[sem] = 16
+        eng[q].dma_start(out, in_).then_inc(T.sem[sem], 16)
+
+    return dict(tt=tt, ts=ts, cp=cp, ms=ms, act=act, iota=iota, sel=sel, mm=mm, dma=dma, wait=wait, deps=deps, known=known,
+                final=final, acc=acc)
+
+
+def plan(src, cores, topo):
+    far = [d for d in cores if d != src and d not in topo.cores_of(src)]
+    near = [d for d in cores if d != src and d in topo.cores_of(src)]
+    eng = topo.engines(src, far[0])
+    rest = [e for e in topo.engines(src, near[0]) if e not in eng]
+    h = len(eng) // 2
+    a = [(d, eng[2 * i:2 * i + 2]) for i, d in enumerate(far[:h])]
+    b = [(d, eng[h * i:h * i + h]) for i, d in enumerate(far[h:])] + [(d, rest) for d in near]
+    return [a, b]
+
+
+def rank_program(g, core, T, topo):
+    rank = T.rank_of(core)
+    if rank is None:
+        return
+    K = make(g, T)
+    tt, ts, cp, ms, act, iota, sel, mm, dma, wait, deps = (K[x] for x in ("tt", "ts", "cp", "ms", "act", "iota", "sel", "mm", "dma", "wait", "deps"))
+
+    def b(n, lo=0, hi=None, st=1):
+        n, at, size = PLACE[n]
+        lo, hi = at + lo, at + (size if hi is None else hi)
+        return (n, lo, hi, st) if st != 1 else (n, lo, hi)
+
+    def col(j):
+        return b("cols", j, j + 1)
+
+    def ind(w, hi, o, lo=0, oh=None):
+        return ("@", (w, 0, hi), b(o, lo, oh))
+
+    def part(x, p0, p1):
+        return (x[0], x[1], x[2], 1, p0, p1)
+
+    fills = []
+
+    def fill(n=1):
+        for _ in range(n):
+            if fills:
+                fills.pop(0)()
+
+    dma("Y", T.Qi[:], T.req[:], w=[b("Qi")])
+    dma("S", T.Ci[:], T.child[:], w=[b("Ci")])
+    dma("Y", T.Ei[:], T.edge[:], w=[b("Ei")])
+    dma("S", T.X[:, 0:1024], T.desc[:, 0:1024], w=[b("X", 0, 1024)])
+    dma("Y", T.X[:, 1024:2048], T.desc[:, 1024:2048], w=[b("X", 1024, 2048)])
+    iota(b("IP"), [[1, 1]], 0, 1)
+    iota(b("IQ"), [[1, 128]], 0, 0)
+    iota(b("C", NDUM, NDUMP), [[1, 128]], NDUM, 0, True)
+    iota(b("N01", 0, 256), [[1, 256]], 384, 0, True)
+    iota(b("N01", 256, 512), [[1, 256]], 640, 0, True)
+    ms(b("L", 384, 1024), 0.0)
+    ts(b("IC", 0, 1), b("IP"), 4, A.arith_shift_right)
+    ts(b("IC", 1, 2), b("IP"), 15, A.bitwise_and)
+    ts(b("IC", 2, 3), b("IP"), 4, A.arith_shift_right, 1, A.bitwise_and)
+    ts(b("R4i", 0, 128), b("IQ"), 4, A.arith_shift_right)
+    ts(b("R4i", 128, 256), b("IQ"), 15, A.bitwise_and)
+    cp(col(0), b("IP"))
+    cp(b("cols", 1, 4), b("IC", 0, 3))
+    cp(b("Qb"), b("IQ"))
+    cp(b("Q4b"), b("R4i"))
+    QMb = b("Q4b", 128, 256)
+    ts(col(5), col(2), 0.0, A.is_equal)
+    ts(col(8), col(0), -1.0, A.add)
+    ts(b("BO"), b("Q4b", 0, 128), col(1), A.is_equal)
+    ts(b("I"), b("Qb"), col(0), A.is_equal)
+    ts(b("MSK"), QMb, col(2), A.is_equal)
+    ts(b("SEL"), b("Qb", 0, 8), col(1), A.is_equal)
+    ts(b("B0"), b("BO"), col(5), A.mult)
+    for n, op, base in (("SHU", A.is_equal, 1), ("TRI", A.is_ge, 0), ("STRI", A.is_gt, 0), ("SHD", A.is_equal, -1)):
+        sel(b(n), b("BO"), [[1, 128]], op, base, -1)
+    for m in range(16):
+        sel(b("CONV", 128 * m, 128 * m + 128), b("BO"), [[0, 8], [1, 16]], A.is_equal, -m, 0)
+    tt(b("DQ"), b("I"), b("SHU"), A.subtract)
+    tt(b("tmpe"), b("I"), b("SHD"), A.subtract)
+    for n, src, c in (("I64", "I", 64.0), ("Im128", "I", -128.0), ("IB", "I", BIG), ("ImB", "I", -BIG), ("I32", "I", 1.0),
+                      ("BO64", "BO", 64.0), ("BOm16", "BO", -16.0), ("BOm1", "BO", -1.0), ("SELB", "SEL", 4096.0),
+                      ("TRI64", "TRI", 64.0), ("D64", "tmpe", 64.0), ("Dm64", "tmpe", -64.0)):
+        act(b(n), b(src), F.Copy, scale=c)
+    ms(b("C", 384, NDUM), 0.0)
+
+    def consts_b():
+        ms(b("KGE"), 1.0)
+        ms(b("BT", 0, 1), -1.0)
+        ts(b("flip"), b("Qb", 0, 16), col(2), A.is_equal, -2.0, A.mult)
+        ts(b("flip"), b("flip"), 1.0, A.add)
+        n = 1
+        for i in range(11):
+            ts(b("BT", n, 2 * n), b("BT", 0, n), b("flip", i, i + 1), A.mult)
+            n *= 2
+        for i in range(4):
+            ts(b("MASKN", 128 * i, 128 * i + 128), b("Qb"), col(0), A.is_le, -64.0, A.mult)
+        ms(b("BAND"), 0.0)
+        ms(b("BAND", 112, 128), 1.0)
+
+    def consts_c():
+        ms(b("ONES"), 1.0)
+        ms(b("Y0"), 1.0)
+        ms(b("Y0", 128, 256), 65.0)
+        ts(b("W8"), b("Qb", 0, 8), 16.0, A.mult, col(2), A.add)
+        for h in (0, 8):
+            ts(b("DUM", h, h + 8), b("W8"), float(NDUM), A.add)
+            ts(b("DD", h, h + 8), b("W8"), float(NDUMP), A.add)
+        ts(b("DTOK"), b("W8"), float(TDUMP), A.add)
+        ts(col(4), col(2), -1.0, A.mult, 15.0, A.add)
+        ts(col(6), col(2), 0.0, A.is_gt)
+
+    def round_start(r):
+        src = b("Qi") if r == 0 else b("LAND0")
+        cp(b("Ql"), src)
+        qi = src
+        if r:
+            qi = b("Qi2")
+            cp(qi, src)
+        ts(b("Q4i"), qi, 4, A.arith_shift_right)
+        ts(b("Q4m"), b("Q4i"), col(5), A.mult)
+        mm([(b("pm", 0, 128), b("Q4m"), b("BO"), True, True)])
+        ts(b("QMi"), qi, 15, A.bitwise_and)
+        cp(b("QM"), b("QMi"))
+        tt(b("mk"), b("pm", 0, 128), b("MSK"), A.mult)
+        mm([(b("pm", 128, 136), b("mk"), b("SEL"), True, True)])
+        mm([(b("ps", 128, 256), b("B0"), b("QM"), True, True)])
+        cp(b("vl"), b("pm", 128, 136))
+        act(b("VC", 0, 8), b("pm", 128, 136), F.Copy)
+        ts(b("OH"), b("ps", 128, 256), col(2), A.is_equal)
+
+    def round_rest(r):
+        src = b("Qi") if r == 0 else b("LAND0")
+        mm([(b("pw", 0, 128), b("DQ"), b("QM"), True, True)])
+        ts(b("P"), b("pw", 0, 128), 16.0, A.add)
+        if r:
+            ms(b("KGE"), 1.0)
+        cp(b("QF"), src)
+        ts(b("uQ"), b("QF"), -1.0, A.mult, 2047.0, A.add)
+
+    def hash_a():
+        cp(b("Q16"), b("QF"))
+        mm([(b("pw", 0, 128), b("SHD"), b("Q16"), True, True)])
+
+    def hash_b():
+        tt(b("HP"), b("pw", 0, 128), b("QF"), A.mult)
+        ts(b("HI"), b("HP"), 5, A.arith_shift_right, 2047, A.bitwise_and)
+        ts(b("HM"), b("HI"), 2046.5, A.is_lt)
+
+    def hash_c():
+        tt(b("HMQ"), b("HI"), b("HM"), A.mult)
+        tt(b("HMQ"), b("HMQ"), b("QF"), A.subtract)
+        ts(b("HMQ"), b("HMQ"), col(6), A.mult)
+
+    def gram_mask(h):
+        mm([(b("pg%d" % h), b("I"), b("MASKN"), True, False)])
+
+    def gram(left, lefto, right, masked):
+        done = {}
+        for y in range(2):
+            for h in range(2):
+                l = []
+                for x in (2 * y, 2 * y + 1):
+                    gr = 4 * h + x
+                    p0 = 32 * (gr // 2)
+                    p1 = p0 + (32 if gr % 2 else 16)
+                    l.append((b("pg%d" % h, 128 * x, 128 * x + 128), part(b(lefto if gr % 2 else left), p0, p1), part(b(right), p0, p1),
+                              not masked, not masked or x == 3))
+                if y:
+                    wait("T", "sT", done[h])
+                done[h] = mm(l)
+
+    def band(gr):
+        return b("BAND", 112 - 16 * gr, 240 - 16 * gr)
+
+    def def_a(r, s):
+        mm([(b("pg0", 0, 256), b("BO"), b("QE%d" % (3 * r + s)), True, True)])
+        if r == 0:
+            mm([(b("pg1", 384, 512), b("BO"), b("BUF", 384, 512), True, True)])
+        cp(b("RI"), b("pg0", 0, 256))
+        ts(b("RA"), b("RI"), 15, A.bitwise_and)
+
+    def def_b(r, s):
+        ts(b("OHc"), b("RA"), col(4), A.is_equal)
+        tt(b("OHN"), b("OHc"), b("N01", 256 * r, 256 * r + 256), A.mult)
+
+    def def_c(r, s):
+        if r == 0:
+            n0 = 384 + 256 * r + 128
+            tt(b("X5"), b("pg1", 384, 512), b("Cc"), A.mult)
+            tt(b("C", n0, n0 + 128), b("C", n0, n0 + 128), b("X5"), A.add)
+        tt(ind("C", 1152, "lc", 8, 16), b("OHN", 0, 128), b("OHN", 128, 256), A.max)
+
+    def unmade(r):
+        n1 = 384 + 256 * r
+        l = []
+        for s in range(S_):
+            q = "QE%d" % (3 * r + s)
+            l += [(b("pg0", 256, 384), b("BO"), b(q, 0, 128), s == 0, False), (b("pg0", 256, 384), b("BOm1"), b(q, 128, 256), False, s == S_ - 1)]
+        mm(l)
+        cp(b("RI", 0, 128), b("pg0", 256, 384))
+        ts(b("RA", 0, 128), b("RI", 0, 128), 15, A.bitwise_and)
+        ts(b("X5"), b("RA", 0, 128), 0.5, A.is_gt)
+        tt(b("L", n1, n1 + 128), b("L", n1, n1 + 128), b("X5"), A.mult)
+
+    def step_a1():
+        tt(b("M1"), ind("C", 1024, "vl"), b("OH"), A.mult)
+        mm([(b("pm", 0, 128), b("M1"), b("BO"), True, True)])
+
+    def step_a2():
+        tt(b("mk"), b("pm", 0, 128), b("MSK"), A.mult)
+        mm([(b("pm", 128, 136), b("mk"), b("SEL"), True, True), (b("pm", 256, 384), b("BO"), b("M1"), True, True)])
+
+    def step_a3():
+        cp(b("cl"), b("pm", 128, 136))
+        act(b("VC", 8, 16), b("pm", 128, 136), F.Copy)
+
+    def step_a4():
+        ts(b("El"), ind("L", 1024, "cl"), -1.0, A.mult, 2047.0, A.add)
+
+    def act_1():
+        act(b("VB"), ind("BT", 1024, "vl"), F.Copy)
+        act(b("VBo"), b("VB"), F.Copy, scale=col(3))
+        gram("VB", "VBo", "VB", True)
+
+    def act_2():
+        act(b("EA", 0, 512), b("pg0"), F.Relu, bias=-15.0)
+        act(b("EA", 512, 1024), b("pg1"), F.Relu, bias=-15.0)
+        mm([(b("pc", 0, 128), band(x), b("EA", 128 * x, 128 * x + 128), x == 0, x == 7) for x in range(8)])
+
+    last = (RO_ - 1, S_ - 1)
+
+    def stood():
+        act(b("CB"), ind("BT", 1024, "cl"), F.Copy)
+        gram("VB", "VBo", "CB", False)
+
+    def xq(q):
+        act(b("XQ", 512 * q, 512 * q + 512), ind("X", 2064, "Ql", 32 * q, 32 * q + 32), F.Copy)
+
+    def df(q):
+        tt(b("DF", 512 * q, 512 * q + 512), ind("X", 2064, "El", 32 * q, 32 * q + 32), b("XQ", 512 * q, 512 * q + 512), A.subtract)
+
+    def ab(q):
+        act(b("AB", 512 * q, 512 * q + 512), b("DF", 512 * q, 512 * q + 512), F.Abs)
+
+    def es(h):
+        ts(b("ES", 512 * h, 512 * h + 512), b("pg%d" % h), 15.5, A.is_gt)
+
+    def shadow(r, leafc):
+        tt(b("CMV"), b("VC", 8, 16), b("VC", 0, 8), A.subtract)
+        tt(b("DMC"), b("DUM", 0, 8), b("VC", 8, 16), A.subtract)
+        tt(b("VCD"), b("VC"), b("DD"), A.subtract)
+        if leafc:
+            tt(b("T1"), b("pm", 256, 384), b("N01", 256 * r + 128, 256 * r + 256), A.subtract)
+            tt(b("T2"), b("T1"), b("OH"), A.mult)
+
+    def step(r, s):
+        leafc = (r, s) != last
+        first = r == 0 and s == 0
+        QE = "QE%d" % (3 * r + s)
+        yF, yL, yC = b("py", 0, 128), b("py", 128, 256), b("py", 256, 384)
+
+        def dist(h):
+            mm([(b("pd", 0, 128), b("ImB"), b("NA"), False, False) if h else (b("pd", 0, 128), b("IB"), b("KGE"), True, False)] + [(b("pd", 64 * h, 64 * h + 64), b("CONV", 128 * k, 128 * k + 128), b("AB", 1024 * h + k, 1024 * h + 1024, 16), False,
+                   h == 1 and k == 15) for k in range(16)])
+
+        def y_pre():
+            mm([(b("py", 0, 384), b("I"), b("Y0"), True, False),
+                (yF, b("Im128"), b("NA"), False, False), (yL, b("Dm64"), b("KGE"), False, False), (yC, b("D64"), b("KGE"), False, False),
+                (yF, b("I64"), b("NN"), False, False), (yL, b("I64"), b("NN"), False, False), (yC, b("I64"), b("NN"), False, False)])
+
+        if s == 0:
+            step_a4()
+            round_rest(r)
+            df(0)
+            ab(0)
+            xq(2)
+            if first:
+                consts_b()
+            for h in range(2):
+                gram_mask(h)
+            act_1()
+            df(1)
+            act_2()
+            xq(3)
+            ab(1)
+            df(2)
+            if first:
+                consts_c()
+            stood()
+            dist(0)
+            fills.extend([hash_a, hash_b, hash_c])
+            df(3)
+            act(b("NA"), b("pc", 0, 128), F.Sign)
+            ab(2)
+            es(0)
+            ab(3)
+            es(1)
+        else:
+            xq(0)
+            xq(1)
+            df(0)
+            ab(0)
+            es(0)
+            xq(2)
+            df(1)
+            ab(1)
+            es(1)
+            dist(0)
+            xq(3)
+            df(2)
+            act(b("NA"), b("pc", 0, 128), F.Sign)
+            ab(2)
+        mm([(b("pc", 128, 256), band(x), b("ES", 128 * x, 128 * x + 128), x == 0, x == 7) for x in range(8)])
+        ts(b("NN"), b("El"), 2047.0, A.is_equal)
+        shadow(r, leafc)
+        y_pre()
+        fill(1)
+        if s:
+            df(3)
+            ab(3)
+        ts(b("STD"), b("pc", 128, 256), 0.5, A.is_gt)
+        mm([(yC, b("I64"), b("STD"), False, False)])
+        dist(1)
+        fill(9)
+        for h in range(2):
+            gram_mask(h)
+        act(b("uE"), ind("L", 1024, "cl"), F.Copy)
+        if leafc:
+            act(b("CV"), ind("C", 1024, "vl"), F.Copy)
+        if r == 0:
+            act(b("Cc"), ind("C", 1024, "cl"), F.Copy)
+        ST, FS, LF, CU = (b("BUF", 128 * i, 128 * i + 128) for i in range(4))
+        ts(ST, b("pd", 0, 128), BIG + 620.5, A.is_gt)
+        mm([(yC, b("STRI"), ST, False, False), (yF, b("STRI"), ST, False, False), (yL, b("STRI"), ST, False, True)])
+        mm([(b("ps", 0, 128), b("TRI64"), ST, True, False)])
+        tt(CU, yC, ST, A.is_le)
+        tt(FS, yF, ST, A.is_le)
+        mm([(b("ps", 0, 128), b("BO64"), FS, False, True)])
+        tt(b(QE, 0, 128), CU, b("uQ"), A.mult)
+        mm([(b("pm", 0, 128), b(QE, 0, 128), b("BO"), True, True)])
+        tt(LF, yL, ST, A.is_le)
+        mm([(b("pw", 0, 32), b("CONV", 128 * m, 128 * m + 128), b("BUF", m, 512, 16), m == 0, m == 15) for m in range(16)])
+        tt(b("mkq", 0, 128), b("pm", 0, 128), b("MSK"), A.mult)
+        mm([(b("pm", 384, 392), b("mkq", 0, 128), b("SEL"), True, True)])
+        if (r, s) != last:
+            tt(b("P"), b("ps", 0, 128), b("P"), A.min)
+            act(b("KGE"), b("P"), F.Sign)
+        if s == S_ - 1:
+            if (r, s) == last:
+                tt(b("KGE"), b("ps", 0, 128), b("KGE"), A.min)
+            tt(b("HK"), b("KGE"), b("HMQ"), A.mult)
+            tt(b("SND"), b("HK"), b("QF"), A.add)
+            travel(r)
+        ts(b("qel", 0, 8), b("pm", 384, 392), -1.0, A.mult, 2047.0, A.add)
+        act(b("QB"), ind("BT", 2048, "qel", 0, 8), F.Copy)
+        tt(b(QE, 128, 256), CU, b("uE"), A.mult)
+        mm([(b("pm", 128, 256), b(QE, 128, 256), b("BO"), True, True)])
+        act(b("QBo"), b("QB"), F.Copy, scale=col(3))
+        gram("QB", "QBo", "QB", True)
+        if s < S_ - 1:
+            mm([(b("ps", 128, 256), b("BO"), b("P"), True, False), (b("ps", 128, 256), b("BOm16"), b("KGE"), False, True)])
+        tt(b("mkq", 128, 256), b("pm", 128, 256), b("MSK"), A.mult)
+        mm([(b("pm", 392, 400), b("mkq", 128, 256), b("SEL"), True, True)])
+        mm([(b("pd", 128, 384), b("TRI"), b("BUF", 256, 512), True, True)])
+        act(b("ED", 0, 512), b("pg0"), F.Relu, bias=-15.0)
+        act(b("ED", 512, 1024), b("pg1"), F.Relu, bias=-15.0)
+        tt(b("l1"), b("pw", 16, 32), b("VCD"), A.mult)
+        tt(b("l2"), b("l1"), b("DD"), A.add)
+        cp(b("lc"), b("l2"))
+        if s < S_ - 1:
+            ts(b("WF"), b("pw", 0, 16), 0.5, A.is_lt)
+            tt(b("w6"), b("pw", 16, 32), b("DUM"), A.mult)
+            tt(b("x1"), b("WF", 0, 8), b("DMC"), A.mult)
+            tt(b("x2"), b("x1"), b("CMV"), A.add)
+            tt(b("x3"), b("WF", 8, 16), b("x2"), A.mult)
+            tt(b("x4"), b("x3"), b("VC", 0, 8), A.add)
+            tt(b("y1"), b("x4"), b("w6", 0, 8), A.max)
+            tt(b("VC", 0, 8), b("y1"), b("w6", 8, 16), A.max)
+            cp(b("vl"), b("VC", 0, 8))
+        ts(b("qel", 8, 16), b("pm", 392, 400), -1.0, A.mult, 2047.0, A.add)
+        act(b("XLg"), ind("X", 2064, "qel", 8, 16), F.Copy)
+        n1 = 384 + 256 * r
+        if leafc:
+            tt(ind("C", 1152, "lc", 0, 8), b("CV"), b("T2"), A.subtract)
+        if s < S_ - 1:
+            ts(b("OH"), b("ps", 128, 256), col(2), A.is_equal)
+            step_a1()
+        mm([(b("pc", 256 + 16 * x, 272 + 16 * x), b("ED", 128 * x, 128 * x + 128), b("ONES", 0, 16), True, True) for x in range(8)])
+        tt(b("X2"), b("pd", 256, 384), b("uE"), A.mult)
+        tt(b("X1"), b("pd", 128, 256), b("uQ"), A.mult)
+        if s < S_ - 1:
+            step_a2()
+        tt(b("X3"), b("pd", 256, 384), b("uQ"), A.mult)
+        tt(b("mk2"), b("pc", 256, 384), b("MSK"), A.mult)
+        mm([(b("pw", 64, 72), b("mk2"), b("SELB"), True, True)])
+        mm([(b("ps", 256, 384), b("I"), b("X3"), True, True), (b("ps", 384, 512), b("I"), b("X1"), True, False),
+            (b("ps", 384, 512), b("I32"), b("X2"), False, True)])
+        cp(b("QLF"), b("qel", 0, 8))
+        if s < S_ - 1:
+            step_a3()
+            for h in range(2):
+                gram_mask(h)
+            act_1()
+            act_2()
+        tt(b("DS"), ind("X", 2064, "qel", 0, 8), b("XLg"), A.add)
+        ts(b("DH"), b("DS"), 1, A.arith_shift_right)
+        tt(b("d1"), b("pw", 64, 72), b("QLF"), A.max)
+        tt(b("d2"), b("d1"), b("DTOK"), A.min)
+        cp(b("didx"), b("d2"))
+        cp(ind("X", 2192, "didx"), b("DH"))
+        if s < S_ - 1:
+            stood()
+        tt(ind("L", 1152, "lc", 8, 16), b("uE"), b("X2"), A.subtract)
+        tt(b("L", n1, n1 + 256), b("ps", 256, 512), b("L", n1, n1 + 256), A.add)
+        if s < S_ - 1:
+            step_a4()
+        if r == 0 or s == 0:
+            fills.extend([lambda: def_a(r, s), lambda: def_b(r, s), lambda: def_c(r, s)])
+        if s == S_ - 1:
+            fill(9)
+            unmade(r)
+
+    sent = [0]
+
+    def travel(r):
+        land = "LAND%d" % r
+        deps("G", [b("SND")], [], "loc", 0)
+        for call in plan(core, T.cores, topo):
+            tr = []
+            for d, en in call:
+                e = (T.rank_of(d) - rank) % 8
+                rid, pid = topo.addr(d, core)
+                tr.append(RemoteDMATransfer(dst_ids=[DstId(rid=rid, pnc=pid)], dma_engine_mask=sum(1 << x for x in en),
+                                            remote_sem=T.sem["arr%d" % r], src=T.SND[:, 16 * e:16 * e + 16],
+                                            dst=T[land][:, 16 * e:16 * e + 16]))
+                sent[0] += len(en)
+            g.remote_dma_fused(tr, local_sem=T.sem.loc)
+        cp(b(land, 0, 16), b("SND", 0, 16))
+        n = sum(len(en) for s in T.cores if s != core for call in plan(s, T.cores, topo) for d, en in call if d == core)
+        K["acc"].setdefault(land, []).append((16, 128, 1, "R", "arr%d" % r, n, True))
+        K["acc"].setdefault("SND", []).append((0, 128, 0, "R", "loc", sent[0], True))
+        K["final"]["arr%d" % r] = n
+        K["final"]["loc"] = sent[0]
+
+    cp(b("C", 0, 384), b("Ci"))
+    for r in range(RO_):
+        round_start(r)
+        step_a1()
+        if r == 0:
+            ts(b("L", 0, 384), b("Ei"), -1.0, A.mult, 2047.0, A.add)
+            cp(b("lsave", 0, 1), b("L", 0, 1))
+            ms(b("L", 0, 1), -1.0)
+            ms(b("X", 2048, 2192), 512.0)
+            cp(b("xsave", 0, 1), b("X", 2047, 2048))
+            ms(b("X", 2047, 2048), 4096.0)
+        xq(0)
+        xq(1)
+        step_a2()
+        step_a3()
+        for s in range(S_):
+            step(r, s)
+    cp(b("X", 2047, 2048), b("xsave", 0, 1))
+    dma("Y", T.yd[:], T.X[:, 0:2048], r=[b("X", 0, 2048)])
+    act(b("YE", 0, 384), b("L", 0, 384), F.Copy, bias=2047.0, scale=-1.0)
+    act(b("YE", 0, 1), b("lsave", 0, 1), F.Copy, bias=2047.0, scale=-1.0)
+    for r in range(RO_):
+        n1 = 384 + 256 * r
+        for j, o in ((128, 0), (0, 1)):
+            act(b("YE", n1 + o, n1 + 256, 2), b("L", n1 + j, n1 + j + 128), F.Copy, bias=2047.0, scale=-1.0)
+    dma("S", T.ye[:], T.YE[:], r=[b("YE")])
+    dma("Y", T.yr[:], T.LAND1[:], r=[b("LAND1")])
+    for s, v in K["final"].items():
+        K["known"]["G"].pop(s, None)
+        wait("G", s, v)

@@ -46,7 +46,7 @@ for _n in range(6):
 _b("CMV", 8, F32); _b("DMC", 8, F32); _b("VCD", 16, F32); _b("WF", 16, F32); _b("x1", 8, F32); _b("x2", 8, F32)
 _b("x3", 8, F32); _b("x4", 8, F32); _b("w6", 16, F32); _b("y1", 8, F32); _b("l1", 16, F32); _b("l2", 16, F32)
 _b("lc", 16, U16); _b("qel", 16, U16); _b("QLF", 8, F32); _b("QB", 128, BF); _b("QBo", 128, BF)
-_b("XLg", 128, F32); _b("DS", 128, I32); _b("DH", 128, I32); _b("mk2", 128, H16); _b("d1", 8, F32); _b("d2", 8, F32)
+_b("XLg", 128, BF); _b("XQg", 128, BF); _b("DS", 128, F32); _b("DH", 128, F32); _b("mk2", 128, H16); _b("d1", 8, F32); _b("d2", 8, F32)
 _b("didx", 8, U16); _b("X1", 128, H16); _b("X2", 128, F32); _b("X3", 128, H16); _b("X5", 128, F32)
 _b("RI", 256, I32); _b("RA", 256, I32); _b("OHc", 256, F32); _b("OHN", 256, F32); _b("YE", 896, F32)
 PS = ["pg0", "pg1", "pc", "pm", "pd", "py", "ps", "pw"]
@@ -257,6 +257,13 @@ def rank_program(g, core, T, topo):
     ts(b("MSK"), QMb, col(2), A.is_equal)
     ts(b("SEL"), b("Qb", 0, 8), col(1), A.is_equal)
     ts(b("B0"), b("BO"), col(5), A.mult)
+    ms(b("BT", 0, 1), -1.0)
+    ts(b("flip"), b("Qb", 0, 16), col(2), A.is_equal, -2.0, A.mult)
+    ts(b("flip"), b("flip"), 1.0, A.add)
+    n = 1
+    for i in range(11):
+        ts(b("BT", n, 2 * n), b("BT", 0, n), b("flip", i, i + 1), A.mult)
+        n *= 2
     for n, op, base in (("SHU", A.is_equal, 1), ("TRI", A.is_ge, 0), ("STRI", A.is_gt, 0), ("SHD", A.is_equal, -1)):
         sel(b(n), b("BO"), [[1, 128]], op, base, -1)
     for m in range(16):
@@ -271,13 +278,6 @@ def rank_program(g, core, T, topo):
 
     def consts_b():
         ms(b("KGE"), 1.0)
-        ms(b("BT", 0, 1), -1.0)
-        ts(b("flip"), b("Qb", 0, 16), col(2), A.is_equal, -2.0, A.mult)
-        ts(b("flip"), b("flip"), 1.0, A.add)
-        n = 1
-        for i in range(11):
-            ts(b("BT", n, 2 * n), b("BT", 0, n), b("flip", i, i + 1), A.mult)
-            n *= 2
         for i in range(4):
             ts(b("MASKN", 128 * i, 128 * i + 128), b("Qb"), col(0), A.is_le, -64.0, A.mult)
         ms(b("BAND"), 0.0)
@@ -300,6 +300,8 @@ def rank_program(g, core, T, topo):
         cp(b("Ql"), src)
         qi = src
         if r:
+            xq(0)
+            xq(1)
             qi = b("Qi2")
             cp(qi, src)
         ts(b("Q4i"), qi, 4, A.arith_shift_right)
@@ -310,13 +312,13 @@ def rank_program(g, core, T, topo):
         tt(b("mk"), b("pm", 0, 128), b("MSK"), A.mult)
         mm([(b("pm", 128, 136), b("mk"), b("SEL"), True, True)])
         mm([(b("ps", 128, 256), b("B0"), b("QM"), True, True)])
+        mm([(b("pw", 0, 128), b("DQ"), b("QM"), True, True)])
         cp(b("vl"), b("pm", 128, 136))
         act(b("VC", 0, 8), b("pm", 128, 136), F.Copy)
         ts(b("OH"), b("ps", 128, 256), col(2), A.is_equal)
 
     def round_rest(r):
         src = b("Qi") if r == 0 else b("LAND0")
-        mm([(b("pw", 0, 128), b("DQ"), b("QM"), True, True)])
         ts(b("P"), b("pw", 0, 128), 16.0, A.add)
         if r:
             ms(b("KGE"), 1.0)
@@ -358,10 +360,12 @@ def rank_program(g, core, T, topo):
     def band(gr):
         return b("BAND", 112 - 16 * gr, 240 - 16 * gr)
 
-    def def_a(r, s):
+    def def_m(r, s):
         mm([(b("pg0", 0, 256), b("BO"), b("QE%d" % (3 * r + s)), True, True)])
         if r == 0:
             mm([(b("pg1", 384, 512), b("BO"), b("BUF", 384, 512), True, True)])
+
+    def def_a(r, s):
         cp(b("RI"), b("pg0", 0, 256))
         ts(b("RA"), b("RI"), 15, A.bitwise_and)
 
@@ -376,13 +380,15 @@ def rank_program(g, core, T, topo):
             tt(b("C", n0, n0 + 128), b("C", n0, n0 + 128), b("X5"), A.add)
         tt(ind("C", 1152, "lc", 8, 16), b("OHN", 0, 128), b("OHN", 128, 256), A.max)
 
-    def unmade(r):
-        n1 = 384 + 256 * r
+    def unmade_m(r):
         l = []
         for s in range(S_):
             q = "QE%d" % (3 * r + s)
             l += [(b("pg0", 256, 384), b("BO"), b(q, 0, 128), s == 0, False), (b("pg0", 256, 384), b("BOm1"), b(q, 128, 256), False, s == S_ - 1)]
         mm(l)
+
+    def unmade(r):
+        n1 = 384 + 256 * r
         cp(b("RI", 0, 128), b("pg0", 256, 384))
         ts(b("RA", 0, 128), b("RI", 0, 128), 15, A.bitwise_and)
         ts(b("X5"), b("RA", 0, 128), 0.5, A.is_gt)
@@ -410,7 +416,7 @@ def rank_program(g, core, T, topo):
 
     def act_2():
         act(b("EA", 0, 512), b("pg0"), F.Relu, bias=-15.0)
-        act(b("EA", 512, 1024), b("pg1"), F.Relu, bias=-15.0)
+        ts(b("EA", 512, 1024), b("pg1"), 15.5, A.is_gt)
         mm([(b("pc", 0, 128), band(x), b("EA", 128 * x, 128 * x + 128), x == 0, x == 7) for x in range(8)])
 
     last = (RO_ - 1, S_ - 1)
@@ -431,13 +437,10 @@ def rank_program(g, core, T, topo):
     def es(h):
         ts(b("ES", 512 * h, 512 * h + 512), b("pg%d" % h), 15.5, A.is_gt)
 
-    def shadow(r, leafc):
+    def words():
         tt(b("CMV"), b("VC", 8, 16), b("VC", 0, 8), A.subtract)
         tt(b("DMC"), b("DUM", 0, 8), b("VC", 8, 16), A.subtract)
         tt(b("VCD"), b("VC"), b("DD"), A.subtract)
-        if leafc:
-            tt(b("T1"), b("pm", 256, 384), b("N01", 256 * r + 128, 256 * r + 256), A.subtract)
-            tt(b("T2"), b("T1"), b("OH"), A.mult)
 
     def step(r, s):
         leafc = (r, s) != last
@@ -458,58 +461,61 @@ def rank_program(g, core, T, topo):
             step_a4()
             round_rest(r)
             df(0)
-            ab(0)
-            xq(2)
-            if first:
-                consts_b()
-            for h in range(2):
-                gram_mask(h)
-            act_1()
-            df(1)
-            act_2()
-            xq(3)
-            ab(1)
-            df(2)
             if first:
                 consts_c()
+            ab(0)
+            act_2()
+            df(1)
+            xq(2)
+            ab(1)
             stood()
+            df(2)
+            xq(3)
+            es(0)
             dist(0)
-            fills.extend([hash_a, hash_b, hash_c])
+            ab(2)
             df(3)
             act(b("NA"), b("pc", 0, 128), F.Sign)
-            ab(2)
-            es(0)
-            ab(3)
             es(1)
+            ab(3)
         else:
             xq(0)
-            xq(1)
             df(0)
+            act_2()
+            xq(1)
             ab(0)
-            es(0)
-            xq(2)
+            stood()
             df(1)
+            xq(2)
             ab(1)
+            es(0)
+            df(2)
             es(1)
             dist(0)
             xq(3)
-            df(2)
             act(b("NA"), b("pc", 0, 128), F.Sign)
             ab(2)
+        if first or (r, s) == last:
+            fills.extend([hash_a, hash_b, hash_c])
+        elif s == 0:
+            fills.extend([lambda: unmade_m(r - 1), lambda: unmade(r - 1)])
+        fill()
         mm([(b("pc", 128, 256), band(x), b("ES", 128 * x, 128 * x + 128), x == 0, x == 7) for x in range(8)])
         ts(b("NN"), b("El"), 2047.0, A.is_equal)
-        shadow(r, leafc)
+        if leafc:
+            tt(b("T1"), b("pm", 256, 384), b("N01", 256 * r + 128, 256 * r + 256), A.subtract)
         y_pre()
-        fill(1)
         if s:
             df(3)
             ab(3)
         ts(b("STD"), b("pc", 128, 256), 0.5, A.is_gt)
         mm([(yC, b("I64"), b("STD"), False, False)])
         dist(1)
+        late = len(fills) > 0
         fill(9)
-        for h in range(2):
-            gram_mask(h)
+        if not late:
+            for h in range(2):
+                gram_mask(h)
         act(b("uE"), ind("L", 1024, "cl"), F.Copy)
         if leafc:
             act(b("CV"), ind("C", 1024, "vl"), F.Copy)
@@ -519,15 +525,22 @@ def rank_program(g, core, T, topo):
         ts(ST, b("pd", 0, 128), BIG + 620.5, A.is_gt)
         mm([(yC, b("STRI"), ST, False, False), (yF, b("STRI"), ST, False, False), (yL, b("STRI"), ST, False, True)])
         mm([(b("ps", 0, 128), b("TRI64"), ST, True, False)])
+        if late:
+            gram_mask(0)
+        words()
         tt(CU, yC, ST, A.is_le)
         tt(FS, yF, ST, A.is_le)
         mm([(b("ps", 0, 128), b("BO64"), FS, False, True)])
+        if late:
+            gram_mask(1)
         tt(b(QE, 0, 128), CU, b("uQ"), A.mult)
         mm([(b("pm", 0, 128), b(QE, 0, 128), b("BO"), True, True)])
         tt(LF, yL, ST, A.is_le)
-        mm([(b("pw", 0, 32), b("CONV", 128 * m, 128 * m + 128), b("BUF", m, 512, 16), m == 0, m == 15) for m in range(16)])
         tt(b("mkq", 0, 128), b("pm", 0, 128), b("MSK"), A.mult)
         mm([(b("pm", 384, 392), b("mkq", 0, 128), b("SEL"), True, True)])
+        mm([(b("pd", 128, 384), b("TRI"), b("BUF", 256, 512), True, True)])
+        mm([(b("pw", 0, 32), b("CONV", 128 * m, 128 * m + 128), b("BUF", m, 512, 16), m == 0, m == 15) for m in range(16)])
+        tt(b(QE, 128, 256), CU, b("uE"), A.mult)
         if (r, s) != last:
             tt(b("P"), b("ps", 0, 128), b("P"), A.min)
             act(b("KGE"), b("P"), F.Sign)
@@ -538,18 +551,25 @@ def rank_program(g, core, T, topo):
             tt(b("SND"), b("HK"), b("QF"), A.add)
             travel(r)
         ts(b("qel", 0, 8), b("pm", 384, 392), -1.0, A.mult, 2047.0, A.add)
+        if leafc:
+            tt(b("T2"), b("T1"), b("OH"), A.mult)
+        tt(b("X2"), b("pd", 256, 384), b("uE"), A.mult)
+        tt(b("X1"), b("pd", 128, 256), b("uQ"), A.mult)
         act(b("QB"), ind("BT", 2048, "qel", 0, 8), F.Copy)
-        tt(b(QE, 128, 256), CU, b("uE"), A.mult)
         mm([(b("pm", 128, 256), b(QE, 128, 256), b("BO"), True, True)])
         act(b("QBo"), b("QB"), F.Copy, scale=col(3))
+        act(b("QLF"), b("pm", 384, 392), F.Copy, bias=2047.0, scale=-1.0)
+        act(b("XQg"), ind("X", 2064, "qel", 0, 8), F.Copy)
         gram("QB", "QBo", "QB", True)
         if s < S_ - 1:
             mm([(b("ps", 128, 256), b("BO"), b("P"), True, False), (b("ps", 128, 256), b("BOm16"), b("KGE"), False, True)])
         tt(b("mkq", 128, 256), b("pm", 128, 256), b("MSK"), A.mult)
         mm([(b("pm", 392, 400), b("mkq", 128, 256), b("SEL"), True, True)])
-        mm([(b("pd", 128, 384), b("TRI"), b("BUF", 256, 512), True, True)])
         act(b("ED", 0, 512), b("pg0"), F.Relu, bias=-15.0)
         act(b("ED", 512, 1024), b("pg1"), F.Relu, bias=-15.0)
+        if s < S_ - 1:
+            for h in range(2):
+                gram_mask(h)
         tt(b("l1"), b("pw", 16, 32), b("VCD"), A.mult)
         tt(b("l2"), b("l1"), b("DD"), A.add)
         cp(b("lc"), b("l2"))
@@ -566,45 +586,41 @@ def rank_program(g, core, T, topo):
         ts(b("qel", 8, 16), b("pm", 392, 400), -1.0, A.mult, 2047.0, A.add)
         act(b("XLg"), ind("X", 2064, "qel", 8, 16), F.Copy)
         n1 = 384 + 256 * r
+        mm([(b("pc", 256 + 16 * x, 272 + 16 * x), b("ED", 128 * x, 128 * x + 128), b("ONES", 0, 16), True, True) for x in range(8)])
         if leafc:
             tt(ind("C", 1152, "lc", 0, 8), b("CV"), b("T2"), A.subtract)
         if s < S_ - 1:
             ts(b("OH"), b("ps", 128, 256), col(2), A.is_equal)
             step_a1()
-        mm([(b("pc", 256 + 16 * x, 272 + 16 * x), b("ED", 128 * x, 128 * x + 128), b("ONES", 0, 16), True, True) for x in range(8)])
-        tt(b("X2"), b("pd", 256, 384), b("uE"), A.mult)
-        tt(b("X1"), b("pd", 128, 256), b("uQ"), A.mult)
         if s < S_ - 1:
             step_a2()
         tt(b("X3"), b("pd", 256, 384), b("uQ"), A.mult)
         tt(b("mk2"), b("pc", 256, 384), b("MSK"), A.mult)
         mm([(b("pw", 64, 72), b("mk2"), b("SELB"), True, True)])
+        mm([(b("pg0", 0, 128) if s == S_ - 1 else b("ps", 128, 256), b("I"), b("XQg"), True, False),
+            (b("pg0", 0, 128) if s == S_ - 1 else b("ps", 128, 256), b("I"), b("XLg"), False, True)])
+        act(b("DS"), b("pg0", 0, 128) if s == S_ - 1 else b("ps", 128, 256), F.Copy, bias=2.0 ** 23, scale=0.5 - 2.0 ** -12)
+        act(b("DH"), b("DS"), F.Copy, bias=-2.0 ** 23)
         mm([(b("ps", 256, 384), b("I"), b("X3"), True, True), (b("ps", 384, 512), b("I"), b("X1"), True, False),
             (b("ps", 384, 512), b("I32"), b("X2"), False, True)])
-        cp(b("QLF"), b("qel", 0, 8))
         if s < S_ - 1:
             step_a3()
-            for h in range(2):
-                gram_mask(h)
             act_1()
-            act_2()
-        tt(b("DS"), ind("X", 2064, "qel", 0, 8), b("XLg"), A.add)
-        ts(b("DH"), b("DS"), 1, A.arith_shift_right)
         tt(b("d1"), b("pw", 64, 72), b("QLF"), A.max)
         tt(b("d2"), b("d1"), b("DTOK"), A.min)
         cp(b("didx"), b("d2"))
         cp(ind("X", 2192, "didx"), b("DH"))
-        if s < S_ - 1:
-            stood()
         tt(ind("L", 1152, "lc", 8, 16), b("uE"), b("X2"), A.subtract)
         tt(b("L", n1, n1 + 256), b("ps", 256, 512), b("L", n1, n1 + 256), A.add)
         if s < S_ - 1:
             step_a4()
         if r == 0 or s == 0:
-            fills.extend([lambda: def_a(r, s), lambda: def_b(r, s), lambda: def_c(r, s)])
+            fills.extend([lambda: def_m(r, s), lambda: def_a(r, s), lambda: def_b(r, s), lambda: def_c(r, s)])
         if s == S_ - 1:
             fill(9)
-            unmade(r)
+            if r == RO_ - 1:
+                unmade_m(r)
+                unmade(r)
 
     sent = [0]
 
@@ -639,10 +655,16 @@ def rank_program(g, core, T, topo):
             ms(b("X", 2048, 2192), 512.0)
             cp(b("xsave", 0, 1), b("X", 2047, 2048))
             ms(b("X", 2047, 2048), 4096.0)
-        xq(0)
-        xq(1)
+            xq(0)
         step_a2()
         step_a3()
+        if r == 0:
+            consts_b()
+        for h in range(2):
+            gram_mask(h)
+        act_1()
+        if r == 0:
+            xq(1)
         for s in range(S_):
             step(r, s)
     cp(b("X", 2047, 2048), b("xsave", 0, 1))

@@ -35,7 +35,7 @@ _b("I32", 128, F32); _b("SEL", 8, BF); _b("SELB", 8, BF); _b("MASKN", 512, BF); 
 _b("W8", 8, F32); _b("DUM", 16, F32); _b("DD", 16, F32); _b("DTOK", 8, F32); _b("N01", 512, F32)
 _b("Qi2", 128, I32); _b("QF", 128, F32); _b("Ql", 128, U16); _b("Q4i", 128, I32); _b("Q4m", 128, H16); _b("QMi", 128, I32)
 _b("QM", 128, H16); _b("uQ", 128, H16); _b("Q16", 128, H16); _b("HP", 128, I32); _b("HI", 128, I32); _b("HM", 128, F32)
-_b("HMQ", 128, F32); _b("HK", 128, F32); _b("SND", 128, F32); _b("LAND0", 128, F32); _b("LAND1", 128, F32)
+_b("HMQ", 128, F32); _b("HK", 128, F32); _b("SND", 128, F32); _b("LQ", 128, F32); _b("LK", 128, BF); _b("LAND1", 128, F32)
 _b("vl", 8, U16); _b("cl", 8, U16); _b("VC", 16, F32); _b("OH", 128, F32); _b("P", 128, BF); _b("KGE", 128, BF)
 _b("M1", 128, H16); _b("mk", 128, H16); _b("mkq", 256, H16); _b("El", 128, U16); _b("XQ", 2048, BF); _b("DF", 2048, BF)
 _b("AB", 2048, BF); _b("VB", 128, BF); _b("VBo", 128, BF); _b("CB", 128, BF); _b("CV", 128, F32); _b("Cc", 128, F32)
@@ -48,11 +48,11 @@ _b("x3", 8, F32); _b("x4", 8, F32); _b("w6", 16, F32); _b("y1", 8, F32); _b("l1"
 _b("lc", 16, U16); _b("qel", 16, U16); _b("QLF", 8, F32); _b("QB", 128, BF); _b("QBo", 128, BF)
 _b("XLg", 128, BF); _b("XQg", 128, BF); _b("DS", 128, F32); _b("DH", 128, F32); _b("mk2", 128, H16); _b("d1", 8, F32); _b("d2", 8, F32)
 _b("didx", 8, U16); _b("X1", 128, H16); _b("X2", 128, F32); _b("X3", 128, H16); _b("X5", 128, F32)
-_b("RI", 256, I32); _b("RA", 256, I32); _b("OHc", 256, F32); _b("OHN", 256, F32); _b("YE", 896, F32)
+_b("RI", 128, I32); _b("RA", 128, I32); _b("RW", 16, I32); _b("RL", 16, U16); _b("IDT", 32, F32); _b("OHc", 256, F32); _b("OHN", 256, F32); _b("YE", 896, F32)
 PS = ["pg0", "pg1", "pc", "pm", "pd", "py", "ps", "pw"]
 for _n in PS:
     _b(_n, 512, F32, "psum")
-SEMAPHORES = ["sV", "sT", "sS", "sG", "loc", "arr0", "arr1"] + ["d%d" % _i for _i in range(12)]
+SEMAPHORES = ["sV", "sT", "sS", "sG", "locE", "loc0", "loc1", "arrE", "arr0", "arr1"] + ["d%d" % _i for _i in range(12)]
 NDUM, NDUMP, TDUMP, BIG = 896, 1024, 2064, float(2 ** 17)
 
 
@@ -237,8 +237,6 @@ def rank_program(g, core, T, topo):
     iota(b("IP"), [[1, 1]], 0, 1)
     iota(b("IQ"), [[1, 128]], 0, 0)
     iota(b("C", NDUM, NDUMP), [[1, 128]], NDUM, 0, True)
-    iota(b("N01", 0, 256), [[1, 256]], 384, 0, True)
-    iota(b("N01", 256, 512), [[1, 256]], 640, 0, True)
     ms(b("L", 384, 1024), 0.0)
     ts(b("IC", 0, 1), b("IP"), 4, A.arith_shift_right)
     ts(b("IC", 1, 2), b("IP"), 15, A.bitwise_and)
@@ -257,27 +255,29 @@ def rank_program(g, core, T, topo):
     ts(b("MSK"), QMb, col(2), A.is_equal)
     ts(b("SEL"), b("Qb", 0, 8), col(1), A.is_equal)
     ts(b("B0"), b("BO"), col(5), A.mult)
-    ms(b("BT", 0, 1), -1.0)
-    ts(b("flip"), b("Qb", 0, 16), col(2), A.is_equal, -2.0, A.mult)
-    ts(b("flip"), b("flip"), 1.0, A.add)
-    n = 1
-    for i in range(11):
-        ts(b("BT", n, 2 * n), b("BT", 0, n), b("flip", i, i + 1), A.mult)
-        n *= 2
     for n, op, base in (("SHU", A.is_equal, 1), ("TRI", A.is_ge, 0), ("STRI", A.is_gt, 0), ("SHD", A.is_equal, -1)):
         sel(b(n), b("BO"), [[1, 128]], op, base, -1)
     for m in range(16):
         sel(b("CONV", 128 * m, 128 * m + 128), b("BO"), [[0, 8], [1, 16]], A.is_equal, -m, 0)
-    tt(b("DQ"), b("I"), b("SHU"), A.subtract)
-    tt(b("tmpe"), b("I"), b("SHD"), A.subtract)
+    iota(b("N01", 0, 256), [[1, 256]], 384, 0, True)
+    iota(b("N01", 256, 512), [[1, 256]], 640, 0, True)
     for n, src, c in (("I64", "I", 64.0), ("Im128", "I", -128.0), ("IB", "I", BIG), ("ImB", "I", -BIG), ("I32", "I", 1.0),
-                      ("BO64", "BO", 64.0), ("BOm16", "BO", -16.0), ("BOm1", "BO", -1.0), ("SELB", "SEL", 4096.0),
-                      ("TRI64", "TRI", 64.0), ("D64", "tmpe", 64.0), ("Dm64", "tmpe", -64.0)):
+                      ("BO64", "BO", 64.0), ("BOm16", "BO", -16.0), ("BOm1", "BO", -1.0), ("SELB", "SEL", 4096.0)):
         act(b(n), b(src), F.Copy, scale=c)
     ms(b("C", 384, NDUM), 0.0)
 
     def consts_b():
         ms(b("KGE"), 1.0)
+        ms(b("BT", 0, 1), -1.0)
+        ts(b("flip"), b("Qb", 0, 16), col(2), A.is_equal, -2.0, A.mult)
+        ts(b("flip"), b("flip"), 1.0, A.add)
+        n = 1
+        for i in range(11):
+            ts(b("BT", n, 2 * n), b("BT", 0, n), b("flip", i, i + 1), A.mult)
+            n *= 2
+        tt(b("tmpe"), b("I"), b("SHD"), A.subtract)
+        for n, src, c in (("TRI64", "TRI", 64.0), ("D64", "tmpe", 64.0), ("Dm64", "tmpe", -64.0)):
+            act(b(n), b(src), F.Copy, scale=c)
         for i in range(4):
             ts(b("MASKN", 128 * i, 128 * i + 128), b("Qb"), col(0), A.is_le, -64.0, A.mult)
         ms(b("BAND"), 0.0)
@@ -294,9 +294,13 @@ def rank_program(g, core, T, topo):
         ts(b("DTOK"), b("W8"), float(TDUMP), A.add)
         ts(col(4), col(2), -1.0, A.mult, 15.0, A.add)
         ts(col(6), col(2), 0.0, A.is_gt)
+        ts(b("IDT", 0, 16), b("Qb", 0, 16), col(4), A.is_equal)
 
     def round_start(r):
-        src = b("Qi") if r == 0 else b("LAND0")
+        src = b("Qi") if r == 0 else b("QF")
+        if r:
+            tt(b("HK"), b("LK"), b("HMQ"), A.mult)
+            tt(b("QF"), b("HK"), b("LQ"), A.add)
         cp(b("Ql"), src)
         qi = src
         if r:
@@ -309,6 +313,8 @@ def rank_program(g, core, T, topo):
         mm([(b("pm", 0, 128), b("Q4m"), b("BO"), True, True)])
         ts(b("QMi"), qi, 15, A.bitwise_and)
         cp(b("QM"), b("QMi"))
+        if r == 0:
+            tt(b("DQ"), b("I"), b("SHU"), A.subtract)
         tt(b("mk"), b("pm", 0, 128), b("MSK"), A.mult)
         mm([(b("pm", 128, 136), b("mk"), b("SEL"), True, True)])
         mm([(b("ps", 128, 256), b("B0"), b("QM"), True, True)])
@@ -318,25 +324,28 @@ def rank_program(g, core, T, topo):
         ts(b("OH"), b("ps", 128, 256), col(2), A.is_equal)
 
     def round_rest(r):
-        src = b("Qi") if r == 0 else b("LAND0")
         ts(b("P"), b("pw", 0, 128), 16.0, A.add)
         if r:
             ms(b("KGE"), 1.0)
-        cp(b("QF"), src)
+        else:
+            cp(b("QF"), b("Qi"))
+            travel("QF", "LQ", "E")
         ts(b("uQ"), b("QF"), -1.0, A.mult, 2047.0, A.add)
 
-    def hash_a():
-        cp(b("Q16"), b("QF"))
+    hsrc = lambda r: b("QF" if r else "LQ")
+
+    def hash_a(r):
+        cp(b("Q16"), hsrc(r))
         mm([(b("pw", 0, 128), b("SHD"), b("Q16"), True, True)])
 
-    def hash_b():
-        tt(b("HP"), b("pw", 0, 128), b("QF"), A.mult)
+    def hash_b(r):
+        tt(b("HP"), b("pw", 0, 128), hsrc(r), A.mult)
         ts(b("HI"), b("HP"), 5, A.arith_shift_right, 2047, A.bitwise_and)
         ts(b("HM"), b("HI"), 2046.5, A.is_lt)
 
-    def hash_c():
+    def hash_c(r):
         tt(b("HMQ"), b("HI"), b("HM"), A.mult)
-        tt(b("HMQ"), b("HMQ"), b("QF"), A.subtract)
+        tt(b("HMQ"), b("HMQ"), hsrc(r), A.subtract)
         ts(b("HMQ"), b("HMQ"), col(6), A.mult)
 
     def gram_mask(h):
@@ -361,23 +370,24 @@ def rank_program(g, core, T, topo):
         return b("BAND", 112 - 16 * gr, 240 - 16 * gr)
 
     def def_m(r, s):
-        mm([(b("pg0", 0, 256), b("BO"), b("QE%d" % (3 * r + s)), True, True)])
         if r == 0:
             mm([(b("pg1", 384, 512), b("BO"), b("BUF", 384, 512), True, True)])
 
     def def_a(r, s):
-        cp(b("RI"), b("pg0", 0, 256))
-        ts(b("RA"), b("RI"), 15, A.bitwise_and)
+        cp(b("RW"), b("pm", 384, 400))
+        ts(b("RW"), b("RW"), 15, A.bitwise_and)
+        cp(b("RL"), b("RW"))
+        for h in range(2):
+            act(b("OHc", 128 * h, 128 * h + 128), ind("IDT", 16, "RL", 8 * h, 8 * h + 8), F.Copy)
 
     def def_b(r, s):
-        ts(b("OHc"), b("RA"), col(4), A.is_equal)
-        tt(b("OHN"), b("OHc"), b("N01", 256 * r, 256 * r + 256), A.mult)
-
-    def def_c(r, s):
         if r == 0:
             n0 = 384 + 256 * r + 128
             tt(b("X5"), b("pg1", 384, 512), b("Cc"), A.mult)
             tt(b("C", n0, n0 + 128), b("C", n0, n0 + 128), b("X5"), A.add)
+        tt(b("OHN"), b("OHc"), b("N01", 256 * r, 256 * r + 256), A.mult)
+
+    def def_c(r, s):
         tt(ind("C", 1152, "lc", 8, 16), b("OHN", 0, 128), b("OHN", 128, 256), A.max)
 
     def unmade_m(r):
@@ -402,9 +412,11 @@ def rank_program(g, core, T, topo):
         tt(b("mk"), b("pm", 0, 128), b("MSK"), A.mult)
         mm([(b("pm", 128, 136), b("mk"), b("SEL"), True, True), (b("pm", 256, 384), b("BO"), b("M1"), True, True)])
 
-    def step_a3():
+    def step_a3(late=False):
         cp(b("cl"), b("pm", 128, 136))
         act(b("VC", 8, 16), b("pm", 128, 136), F.Copy)
+        if not late:
+            act(b("CB"), ind("BT", 1024, "cl"), F.Copy)
 
     def step_a4():
         ts(b("El"), ind("L", 1024, "cl"), -1.0, A.mult, 2047.0, A.add)
@@ -414,9 +426,11 @@ def rank_program(g, core, T, topo):
         act(b("VBo"), b("VB"), F.Copy, scale=col(3))
         gram("VB", "VBo", "VB", True)
 
-    def act_2():
+    def act_2(stand=False):
         act(b("EA", 0, 512), b("pg0"), F.Relu, bias=-15.0)
         ts(b("EA", 512, 1024), b("pg1"), 15.5, A.is_gt)
+        if stand:
+            gram("VB", "VBo", "CB", False)
         mm([(b("pc", 0, 128), band(x), b("EA", 128 * x, 128 * x + 128), x == 0, x == 7) for x in range(8)])
 
     last = (RO_ - 1, S_ - 1)
@@ -446,45 +460,63 @@ def rank_program(g, core, T, topo):
         leafc = (r, s) != last
         first = r == 0 and s == 0
         QE = "QE%d" % (3 * r + s)
-        yF, yL, yC = b("py", 0, 128), b("py", 128, 256), b("py", 256, 384)
+        yF, yL, yC = b("py", 0, 128), b("py", 128, 256), b("pm", 256, 384)
 
         def dist(h):
             mm([(b("pd", 0, 128), b("ImB"), b("NA"), False, False) if h else (b("pd", 0, 128), b("IB"), b("KGE"), True, False)] + [(b("pd", 64 * h, 64 * h + 64), b("CONV", 128 * k, 128 * k + 128), b("AB", 1024 * h + k, 1024 * h + 1024, 16), False,
                    h == 1 and k == 15) for k in range(16)])
 
         def y_pre():
-            mm([(b("py", 0, 384), b("I"), b("Y0"), True, False),
-                (yF, b("Im128"), b("NA"), False, False), (yL, b("Dm64"), b("KGE"), False, False), (yC, b("D64"), b("KGE"), False, False),
-                (yF, b("I64"), b("NN"), False, False), (yL, b("I64"), b("NN"), False, False), (yC, b("I64"), b("NN"), False, False)])
+            mm([(b("py", 0, 256), b("I"), b("Y0", 0, 256), True, False),
+                (yF, b("Im128"), b("NA"), False, False), (yL, b("Dm64"), b("KGE"), False, False),
+                (yF, b("I64"), b("NN"), False, False), (yL, b("I64"), b("NN"), False, False)])
+            mm([(yC, b("I"), b("Y0", 0, 128), True, False), (yC, b("D64"), b("KGE"), False, False), (yC, b("I64"), b("NN"), False, False)])
 
         if s == 0:
             step_a4()
             round_rest(r)
-            df(0)
-            if first:
-                consts_c()
-            ab(0)
-            act_2()
-            df(1)
             xq(2)
-            ab(1)
-            stood()
-            df(2)
-            xq(3)
-            es(0)
-            dist(0)
-            ab(2)
-            df(3)
-            act(b("NA"), b("pc", 0, 128), F.Sign)
-            es(1)
-            ab(3)
+            df(0)
+            ab(0)
+            if first:
+                xq(3)
+                consts_b()
+                for h in range(2):
+                    gram_mask(h)
+                act_1()
+                df(1)
+                ab(1)
+                df(2)
+                act_2()
+                stood()
+                consts_c()
+                ab(2)
+                df(3)
+                ab(3)
+                dist(0)
+                act(b("NA"), b("pc", 0, 128), F.Sign)
+                es(0)
+                es(1)
+            else:
+                act_2()
+                df(1)
+                xq(3)
+                ab(1)
+                stood()
+                df(2)
+                dist(0)
+                ab(2)
+                df(3)
+                es(0)
+                act(b("NA"), b("pc", 0, 128), F.Sign)
+                es(1)
+                ab(3)
         else:
             xq(0)
             df(0)
-            act_2()
+            act_2(True)
             xq(1)
             ab(0)
-            stood()
             df(1)
             xq(2)
             ab(1)
@@ -495,11 +527,14 @@ def rank_program(g, core, T, topo):
             xq(3)
             act(b("NA"), b("pc", 0, 128), F.Sign)
             ab(2)
-        if first or (r, s) == last:
-            fills.extend([hash_a, hash_b, hash_c])
-        elif s == 0:
+            if len(fills) == 4:
+                fill(2)
+        if (r, s) == last:
+            fills.extend([lambda: hash_a(r), lambda: hash_b(r), lambda: hash_c(r)])
+        elif s == 0 and r:
             fills.extend([lambda: unmade_m(r - 1), lambda: unmade(r - 1)])
-        fill()
+        if len(fills) > 2 or s == 0:
+            fill()
         mm([(b("pc", 128, 256), band(x), b("ES", 128 * x, 128 * x + 128), x == 0, x == 7) for x in range(8)])
         ts(b("NN"), b("El"), 2047.0, A.is_equal)
         if leafc:
@@ -523,40 +558,43 @@ def rank_program(g, core, T, topo):
             act(b("Cc"), ind("C", 1024, "cl"), F.Copy)
         ST, FS, LF, CU = (b("BUF", 128 * i, 128 * i + 128) for i in range(4))
         ts(ST, b("pd", 0, 128), BIG + 620.5, A.is_gt)
-        mm([(yC, b("STRI"), ST, False, False), (yF, b("STRI"), ST, False, False), (yL, b("STRI"), ST, False, True)])
+        mm([(yC, b("STRI"), ST, False, True)])
+        mm([(yF, b("STRI"), ST, False, False), (yL, b("STRI"), ST, False, True)])
         mm([(b("ps", 0, 128), b("TRI64"), ST, True, False)])
         if late:
             gram_mask(0)
         words()
         tt(CU, yC, ST, A.is_le)
+        tt(b(QE, 0, 128), CU, b("uQ"), A.mult)
+        mm([(b("pm", 0, 128), b(QE, 0, 128), b("BO"), True, True)])
         tt(FS, yF, ST, A.is_le)
         mm([(b("ps", 0, 128), b("BO64"), FS, False, True)])
         if late:
             gram_mask(1)
-        tt(b(QE, 0, 128), CU, b("uQ"), A.mult)
-        mm([(b("pm", 0, 128), b(QE, 0, 128), b("BO"), True, True)])
         tt(LF, yL, ST, A.is_le)
         tt(b("mkq", 0, 128), b("pm", 0, 128), b("MSK"), A.mult)
         mm([(b("pm", 384, 392), b("mkq", 0, 128), b("SEL"), True, True)])
         mm([(b("pd", 128, 384), b("TRI"), b("BUF", 256, 512), True, True)])
-        mm([(b("pw", 0, 32), b("CONV", 128 * m, 128 * m + 128), b("BUF", m, 512, 16), m == 0, m == 15) for m in range(16)])
         tt(b(QE, 128, 256), CU, b("uE"), A.mult)
+        mm([(b("pm", 128, 256), b(QE, 128, 256), b("BO"), True, True)])
+        mm([(b("pw", 0, 32), b("CONV", 128 * m, 128 * m + 128), b("BUF", m, 512, 16), m == 0, m == 15) for m in range(16)])
         if (r, s) != last:
             tt(b("P"), b("ps", 0, 128), b("P"), A.min)
             act(b("KGE"), b("P"), F.Sign)
-        if s == S_ - 1:
-            if (r, s) == last:
-                tt(b("KGE"), b("ps", 0, 128), b("KGE"), A.min)
+        if (r, s) == last:
+            tt(b("KGE"), b("ps", 0, 128), b("KGE"), A.min)
+        ts(b("qel", 0, 8), b("pm", 384, 392), -1.0, A.mult, 2047.0, A.add)
+        if (r, s) == last:
             tt(b("HK"), b("KGE"), b("HMQ"), A.mult)
             tt(b("SND"), b("HK"), b("QF"), A.add)
-            travel(r)
-        ts(b("qel", 0, 8), b("pm", 384, 392), -1.0, A.mult, 2047.0, A.add)
+            travel("SND", "LAND1", "1")
+        elif s == S_ - 1:
+            travel("KGE", "LK", "0")
         if leafc:
             tt(b("T2"), b("T1"), b("OH"), A.mult)
         tt(b("X2"), b("pd", 256, 384), b("uE"), A.mult)
         tt(b("X1"), b("pd", 128, 256), b("uQ"), A.mult)
         act(b("QB"), ind("BT", 2048, "qel", 0, 8), F.Copy)
-        mm([(b("pm", 128, 256), b(QE, 128, 256), b("BO"), True, True)])
         act(b("QBo"), b("QB"), F.Copy, scale=col(3))
         act(b("QLF"), b("pm", 384, 392), F.Copy, bias=2047.0, scale=-1.0)
         act(b("XQg"), ind("X", 2064, "qel", 0, 8), F.Copy)
@@ -592,24 +630,31 @@ def rank_program(g, core, T, topo):
         if s < S_ - 1:
             ts(b("OH"), b("ps", 128, 256), col(2), A.is_equal)
             step_a1()
+        mm([(b("ps", 128, 256), b("I"), b("XQg"), True, False), (b("ps", 128, 256), b("I"), b("XLg"), False, True)])
+        act(b("DS"), b("ps", 128, 256), F.Copy, bias=2.0 ** 23, scale=0.5 - 2.0 ** -12)
+        act(b("DH"), b("DS"), F.Copy, bias=-2.0 ** 23)
         if s < S_ - 1:
             step_a2()
         tt(b("X3"), b("pd", 256, 384), b("uQ"), A.mult)
+        if s == S_ - 1 and r == 0:
+            hash_a(r)
+            hash_b(r)
         tt(b("mk2"), b("pc", 256, 384), b("MSK"), A.mult)
         mm([(b("pw", 64, 72), b("mk2"), b("SELB"), True, True)])
-        mm([(b("pg0", 0, 128) if s == S_ - 1 else b("ps", 128, 256), b("I"), b("XQg"), True, False),
-            (b("pg0", 0, 128) if s == S_ - 1 else b("ps", 128, 256), b("I"), b("XLg"), False, True)])
-        act(b("DS"), b("pg0", 0, 128) if s == S_ - 1 else b("ps", 128, 256), F.Copy, bias=2.0 ** 23, scale=0.5 - 2.0 ** -12)
-        act(b("DH"), b("DS"), F.Copy, bias=-2.0 ** 23)
         mm([(b("ps", 256, 384), b("I"), b("X3"), True, True), (b("ps", 384, 512), b("I"), b("X1"), True, False),
             (b("ps", 384, 512), b("I32"), b("X2"), False, True)])
         if s < S_ - 1:
             step_a3()
             act_1()
+        if s == S_ - 1 and r == 0:
+            hash_c(r)
         tt(b("d1"), b("pw", 64, 72), b("QLF"), A.max)
         tt(b("d2"), b("d1"), b("DTOK"), A.min)
         cp(b("didx"), b("d2"))
         cp(ind("X", 2192, "didx"), b("DH"))
+        if (r, s) == last:
+            cp(b("X", 2047, 2048), b("xsave", 0, 1))
+            dma("Y", T.yd[:], T.X[:, 0:2048], r=[b("X", 0, 2048)])
         tt(ind("L", 1152, "lc", 8, 16), b("uE"), b("X2"), A.subtract)
         tt(b("L", n1, n1 + 256), b("ps", 256, 512), b("L", n1, n1 + 256), A.add)
         if s < S_ - 1:
@@ -618,35 +663,34 @@ def rank_program(g, core, T, topo):
             fills.extend([lambda: def_m(r, s), lambda: def_a(r, s), lambda: def_b(r, s), lambda: def_c(r, s)])
         if s == S_ - 1:
             fill(9)
-            if r == RO_ - 1:
-                unmade_m(r)
-                unmade(r)
+        if (r, s) == last:
+            unmade_m(r)
+            unmade(r)
 
-    sent = [0]
-
-    def travel(r):
-        land = "LAND%d" % r
-        deps("G", [b("SND")], [], "loc", 0)
+    def travel(src, land, tag):
+        sent = [0]
+        deps("G", [b(src)], [], "loc" + tag, 0)
         for call in plan(core, T.cores, topo):
             tr = []
             for d, en in call:
                 e = (T.rank_of(d) - rank) % 8
                 rid, pid = topo.addr(d, core)
                 tr.append(RemoteDMATransfer(dst_ids=[DstId(rid=rid, pnc=pid)], dma_engine_mask=sum(1 << x for x in en),
-                                            remote_sem=T.sem["arr%d" % r], src=T.SND[:, 16 * e:16 * e + 16],
+                                            remote_sem=T.sem["arr" + tag], src=T[src][:, 16 * e:16 * e + 16],
                                             dst=T[land][:, 16 * e:16 * e + 16]))
                 sent[0] += len(en)
-            g.remote_dma_fused(tr, local_sem=T.sem.loc)
-        cp(b(land, 0, 16), b("SND", 0, 16))
+            g.remote_dma_fused(tr, local_sem=T.sem["loc" + tag])
+        cp(b(land, 0, 16), b(src, 0, 16))
         n = sum(len(en) for s in T.cores if s != core for call in plan(s, T.cores, topo) for d, en in call if d == core)
-        K["acc"].setdefault(land, []).append((16, 128, 1, "R", "arr%d" % r, n, True))
-        K["acc"].setdefault("SND", []).append((0, 128, 0, "R", "loc", sent[0], True))
-        K["final"]["arr%d" % r] = n
-        K["final"]["loc"] = sent[0]
+        K["acc"].setdefault(land, []).append((16, 128, 1, "R", "arr" + tag, n, True))
+        K["acc"].setdefault(src, []).append((0, 128, 0, "R", "loc" + tag, sent[0], True))
+        K["final"]["arr" + tag] = n
+        K["final"]["loc" + tag] = sent[0]
 
-    cp(b("C", 0, 384), b("Ci"))
     for r in range(RO_):
         round_start(r)
+        if r == 0:
+            cp(b("C", 0, 384), b("Ci"))
         step_a1()
         if r == 0:
             ts(b("L", 0, 384), b("Ei"), -1.0, A.mult, 2047.0, A.add)
@@ -657,18 +701,15 @@ def rank_program(g, core, T, topo):
             ms(b("X", 2047, 2048), 4096.0)
             xq(0)
         step_a2()
-        step_a3()
-        if r == 0:
-            consts_b()
-        for h in range(2):
-            gram_mask(h)
-        act_1()
+        step_a3(True)
         if r == 0:
             xq(1)
+        else:
+            for h in range(2):
+                gram_mask(h)
+            act_1()
         for s in range(S_):
             step(r, s)
-    cp(b("X", 2047, 2048), b("xsave", 0, 1))
-    dma("Y", T.yd[:], T.X[:, 0:2048], r=[b("X", 0, 2048)])
     act(b("YE", 0, 384), b("L", 0, 384), F.Copy, bias=2047.0, scale=-1.0)
     act(b("YE", 0, 1), b("lsave", 0, 1), F.Copy, bias=2047.0, scale=-1.0)
     for r in range(RO_):

from concourse.bass import DstId, RemoteDMATransfer
from concourse.mybir import AluOpType as A, ActivationFunctionType as F

S_, RO_ = 3, 2
F32, BF, H16, I32, U16 = "float32", "bfloat16", "float16", "int32", "uint16"
SCRATCH = {}


PLACE = {}


def _b(name, n, d, where="sbuf"):
    pool = {F32: "poolf", U16: "poolu", I32: "pooli"}.get(d)
    if name.startswith("QE"):
        pool = "poolq"
    elif n > 16 or where != "sbuf":
        pool = None
    if pool is None:
        SCRATCH[name] = (where, [128, n], d)
        PLACE[name] = (name, 0, n)
    else:
        at = SCRATCH[pool][1][1] if pool in SCRATCH else 0
        SCRATCH[pool] = ("sbuf", [128, at + n + n % 2], d)
        PLACE[name] = (pool, at, n)


_b("X", 2192, BF); _b("L", 1152, F32); _b("C", 1152, F32); _b("BT", 2048, BF)
_b("Ei", 384, I32); _b("Ci", 384, I32); _b("Qi", 128, I32); _b("xsave", 16, BF); _b("lsave", 4, F32)
_b("IQ", 128, I32); _b("IP", 1, I32); _b("IC", 4, I32); _b("R4i", 256, I32); _b("Qb", 128, BF); _b("Q4b", 256, BF)
_b("cols", 16, F32); _b("flip", 16, F32); _b("BO", 128, BF); _b("R", 128, BF); _b("CONV", 2048, BF)
for _n in ("I", "TRI", "STRI", "SHD", "SHU", "D64", "Dm64", "DQ", "I64", "Im128", "IB", "ImB", "TRI64", "BO64", "BOm16", "BOm1",
           "MSK", "B0", "ONES", "tmpc", "tmpd", "tmpe"):
    _b(_n, 128, BF)
_b("I32", 128, F32); _b("SEL", 8, BF); _b("SELB", 8, BF); _b("MASKN", 512, BF); _b("BAND", 240, BF); _b("Y0", 384, BF)
_b("W8", 8, F32); _b("DUM", 16, F32); _b("DD", 16, F32); _b("DTOK", 8, F32); _b("N01", 512, F32)
_b("Qi2", 128, I32); _b("QF", 128, F32); _b("Ql", 128, U16); _b("Q4i", 128, I32); _b("Q4m", 128, H16); _b("QMi", 128, I32)
_b("QM", 128, H16); _b("uQ", 128, H16); _b("Q16", 128, H16); _b("HP", 128, I32); _b("HI", 128, I32); _b("HM", 128, F32)
_b("HMQ", 128, F32); _b("HK", 128, F32); _b("SND", 128, F32); _b("LQ", 128, F32); _b("LK", 128, BF); _b("LAND1", 128, F32)
_b("vl", 8, U16); _b("cl", 8, U16); _b("VC", 16, F32); _b("OH", 128, F32); _b("P", 128, BF); _b("KGE", 128, BF)
_b("M1", 128, H16); _b("mk", 128, H16); _b("mkq", 256, H16); _b("El", 128, U16); _b("XQ", 2048, BF); _b("DF", 2048, BF)
_b("AB", 2048, BF); _b("VB", 128, BF); _b("VBo", 128, BF); _b("CB", 128, BF); _b("CV", 128, F32); _b("Cc", 128, F32)
_b("uE", 128, F32); _b("EA", 1024, BF); _b("ED", 1024, BF); _b("ES", 1024, BF); _b("NA", 128, BF); _b("STD", 128, BF)
_b("NN", 128, BF); _b("T1", 128, F32); _b("T2", 128, F32); _b("BUF", 512, H16)
for _n in range(6):
    _b("QE%d" % _n, 256, H16)
_b("CMV", 8, F32); _b("DMC", 8, F32); _b("VCD", 16, F32); _b("WF", 16, F32); _b("x1", 8, F32); _b("x2", 8, F32)
_b("x3", 8, F32); _b("x4", 8, F32); _b("w6", 16, F32); _b("y1", 8, F32); _b("l1", 16, F32); _b("l2", 16, F32)
_b("lc", 16, U16); _b("qel", 16, U16); _b("QLF", 8, F32); _b("QB", 128, BF); _b("QBo", 128, BF)
_b("XLg", 128, BF); _b("XQg", 128, BF); _b("DS", 128, F32); _b("DH", 128, F32); _b("mk2", 128, H16); _b("d1", 8, F32); _b("d2", 8, F32)
_b("didx", 8, U16); _b("X1", 128, H16); _b("X2", 128, F32); _b("X3", 128, H16); _b("X5", 128, F32)
_b("RI", 128, I32); _b("RA", 128, I32); _b("RW", 16, I32); _b("RL", 16, U16); _b("IDT", 32, F32); _b("OHc", 256, F32); _b("OHN", 256, F32); _b("YE", 896, F32)
PS = ["pg0", "pg1", "pc", "pm", "pd", "py", "ps", "pw"]
for _n in PS:
    _b(_n, 512, F32, "psum")
SEMAPHORES = ["sV", "sT", "sS", "sG", "locE", "loc0", "loc1", "arrE", "arr0", "arr1"] + ["d%d" % _i for _i in range(12)]
NDUM, NDUMP, TDUMP, BIG = 896, 1024, 2064, float(2 ** 17)


def make(g, T):
    eng = {"V": g.vector, "S": g.scalar, "T": g.tensor, "G": g, "Y": g.sync}
    tick = {"V": 0, "S": 0, "T": 0, "G": 0}
    known = {q: {} for q in eng}
    snap, acc, final, ndma = {}, {}, {}, [0]

    def ap(x):
        if x[0] == "@":
            return ap(x[1]).indirect(ap(x[2]))
        t = T[x[0]]
        st = x[3] if len(x) > 3 else 1
        p0, p1 = (x[4], x[5]) if len(x) > 4 else (0, 128)
        return t[p0:p1, x[1]:x[2]:st] if st != 1 else t[p0:p1, x[1]:x[2]]

    def flat(xs):
        out = []
        for x in xs:
            if x is None or isinstance(x, (int, float)):
                continue
            if x[0] == "@":
                out += [x[1], x[2]]
            else:
                out.append(x)
        return out

    def wait(q, sem, val):
        k = known[q]
        if k.get(sem, 0) >= val:
            return
        eng[q].wait_ge(T.sem[sem], val)
        k[sem] = val
        for s, v in snap.get((sem, val), {}).items():
            if k.get(s, 0) < v:
                k[s] = v

    def deps(q, reads, writes, sem, val, dma=False):
        need = {}
        for isw, xs in ((0, reads), (1, writes)):
            for x in xs:
                n, lo, hi = x[0], x[1], x[2]
                ps = n in PS
                for e in acc.get(n, []):
                    elo, ehi, ew, eq, es, ev, ed = e
                    if ps:
                        if eq == q and (q == "T" or not (isw or ew) or ehi <= lo or hi <= elo):
                            continue
                    else:
                        if ehi <= lo or hi <= elo or not (isw or ew):
                            continue
                    need[es] = max(need.get(es, 0), ev)
        for s in sorted(need, key=lambda z: z == "s" + q):
            wait(q, s, need[s])
        for isw, xs in ((0, reads), (1, writes)):
            for x in xs:
                n, lo, hi = x[0], x[1], x[2]
                full = len(x) < 5
                l = acc.setdefault(n, [])
                if isw and full and n not in PS and (len(x) < 4 or x[3] == 1):
                    l[:] = [e for e in l if not (lo <= e[0] and e[1] <= hi)]
                else:
                    l[:] = [e for e in l if not (e[3] == q and not e[6] and not dma and e[0] == lo and e[1] == hi and e[2] == isw)]
                l.append((lo, hi, isw, q, sem, val, dma))

    def fin(q, ins):
        sem = "s" + q
        tick[q] += 1
        snap[(sem, tick[q])] = dict(known[q])
        final[sem] = tick[q]
        ins.then_inc(T.sem[sem], 1)

    def pre(q, reads, writes):
        deps(q, flat(reads), flat(writes), "s" + q, tick[q] + 1)

    def wr(out):
        return ([out[1]], [out[2]]) if out[0] == "@" else ([out], [])

    def tt(out, a, b, op):
        w, r = wr(out)
        pre("V", [a, b] + r, w)
        fin("V", g.vector.tensor_tensor(ap(out), ap(a), ap(b), op))

    def ts(out, a, s1, op0, s2=None, op1=None):
        pre("V", [a, s1, s2], [out])
        f = lambda s: ap(s) if isinstance(s, tuple) else s
        if op1 is None:
            fin("V", g.vector.tensor_scalar(ap(out), ap(a), f(s1), None, op0))
        else:
            fin("V", g.vector.tensor_scalar(ap(out), ap(a), f(s1), f(s2), op0, op1))

    def cp(out, a):
        w, r = wr(out)
        pre("V", [a] + r, w)
        fin("V", g.vector.tensor_copy(ap(out), ap(a)))

    def ms(out, c):
        pre("V", [], [out])
        fin("V", g.vector.memset(ap(out), c))

    def act(out, a, func, bias=0.0, scale=1.0):
        pre("S", [a, scale], [out])
        sc = ap(scale) if isinstance(scale, tuple) else scale
        fin("S", g.scalar.activation(ap(out), ap(a), func, bias=bias, scale=sc))

    def iota(out, pattern, base, cm, fl=False):
        pre("G", [], [out])
        if fl:
            fin("G", g.iota(ap(out), pattern, base, cm, allow_small_or_imprecise_dtypes=True))
        else:
            fin("G", g.iota(ap(out), pattern, base, cm))

    def sel(out, a, pattern, op, base, cm):
        pre("G", [a], [out])
        fin("G", g.affine_select(ap(out), ap(a), pattern, op, 0.0, base, cm))

    def mm(lst):
        pre("T", [x[1] for x in lst] + [x[2] for x in lst], [x[0] for x in lst])
        for i, (o, l, r, st, sp) in enumerate(lst):
            ins = g.tensor.matmul(ap(o), ap(l), ap(r), st, sp)
            if i == len(lst) - 1:
                fin("T", ins)
        return tick["T"]

    def dma(q, out, in_, r=(), w=()):
        sem = "d%d" % ndma[0]
        ndma[0] += 1
        deps(q, list(r), list(w), sem, 16, True)
        snap[(sem, 16)] = dict(known[q])
        final[sem] = 16
        eng[q].dma_start(out, in_).then_inc(T.sem[sem], 16)

    return dict(tt=tt, ts=ts, cp=cp, ms=ms, act=act, iota=iota, sel=sel, mm=mm, dma=dma, wait=wait, deps=deps, known=known,
                final=final, acc=acc)


def plan(src, cores, topo):
    far = [d for d in cores if d != src and d not in topo.cores_of(src)]
    near = [d for d in cores if d != src and d in topo.cores_of(src)]
    eng = topo.engines(src, far[0])
    rest = [e for e in topo.engines(src, near[0]) if e not in eng]
    h = len(eng) // 2
    a = [(d, eng[2 * i:2 * i + 2]) for i, d in enumerate(far[:h])]
    b = [(d, eng[h * i:h * i + h]) for i, d in enumerate(far[h:])] + [(d, rest) for d in near]
    return [a, b]


def rank_program(g, core, T, topo):
    rank = T.rank_of(core)
    if rank is None:
        return
    K = make(g, T)
    tt, ts, cp, ms, act, iota, sel, mm, dma, wait, deps = (K[x] for x in ("tt", "ts", "cp", "ms", "act", "iota", "sel", "mm", "dma", "wait", "deps"))

    def b(n, lo=0, hi=None, st=1):
        n, at, size = PLACE[n]
        lo, hi = at + lo, at + (size if hi is None else hi)
        return (n, lo, hi, st) if st != 1 else (n, lo, hi)

    def col(j):
        return b("cols", j, j + 1)

    def ind(w, hi, o, lo=0, oh=None):
        return ("@", (w, 0, hi), b(o, lo, oh))

    def part(x, p0, p1):
        return (x[0], x[1], x[2], 1, p0, p1)

    fills = []

    def fill(n=1):
        for _ in range(n):
            if fills:
                fills.pop(0)()

    dma("Y", T.Qi[:], T.req[:], w=[b("Qi")])
    dma("S", T.Ci[:], T.child[:], w=[b("Ci")])
    dma("Y", T.Ei[:], T.edge[:], w=[b("Ei")])
    dma("S", T.X[:, 0:1024], T.desc[:, 0:1024], w=[b("X", 0, 1024)])
    dma("Y", T.X[:, 1024:2048], T.desc[:, 1024:2048], w=[b("X", 1024, 2048)])
    iota(b("IP"), [[1, 1]], 0, 1)
    iota(b("IQ"), [[1, 128]], 0, 0)
    iota(b("C", NDUM, NDUMP), [[1, 128]], NDUM, 0, True)
    ms(b("L", 384, 1024), 0.0)
    ts(b("IC", 0, 1), b("IP"), 4, A.arith_shift_right)
    ts(b("IC", 1, 2), b("IP"), 15, A.bitwise_and)
    ts(b("IC", 2, 3), b("IP"), 4, A.arith_shift_right, 1, A.bitwise_and)
    ts(b("R4i", 0, 128), b("IQ"), 4, A.arith_shift_right)
    ts(b("R4i", 128, 256), b("IQ"), 15, A.bitwise_and)
    cp(col(0), b("IP"))
    cp(b("cols", 1, 4), b("IC", 0, 3))
    cp(b("Qb"), b("IQ"))
    cp(b("Q4b"), b("R4i"))
    QMb = b("Q4b", 128, 256)
    ts(col(5), col(2), 0.0, A.is_equal)
    ts(col(8), col(0), -1.0, A.add)
    ts(b("BO"), b("Q4b", 0, 128), col(1), A.is_equal)
    ts(b("I"), b("Qb"), col(0), A.is_equal)
    ts(b("MSK"), QMb, col(2), A.is_equal)
    ts(b("SEL"), b("Qb", 0, 8), col(1), A.is_equal)
    ts(b("B0"), b("BO"), col(5), A.mult)
    for n, op, base in (("SHU", A.is_equal, 1), ("TRI", A.is_ge, 0), ("STRI", A.is_gt, 0), ("SHD", A.is_equal, -1)):
        sel(b(n), b("BO"), [[1, 128]], op, base, -1)
    for m in range(16):
        sel(b("CONV", 128 * m, 128 * m + 128), b("BO"), [[0, 8], [1, 16]], A.is_equal, -m, 0)
    iota(b("N01", 0, 256), [[1, 256]], 384, 0, True)
    iota(b("N01", 256, 512), [[1, 256]], 640, 0, True)
    for n, src, c in (("I64", "I", 64.0), ("Im128", "I", -128.0), ("IB", "I", BIG), ("ImB", "I", -BIG), ("I32", "I", 1.0),
                      ("BO64", "BO", 64.0), ("BOm16", "BO", -16.0), ("BOm1", "BO", -1.0), ("SELB", "SEL", 4096.0)):
        act(b(n), b(src), F.Copy, scale=c)
    ms(b("C", 384, NDUM), 0.0)

    def consts_b():
        ms(b("KGE"), 1.0)
        ms(b("BT", 0, 1), -1.0)
        ts(b("flip"), b("Qb", 0, 16), col(2), A.is_equal, -2.0, A.mult)
        ts(b("flip"), b("flip"), 1.0, A.add)
        n = 1
        for i in range(11):
            ts(b("BT", n, 2 * n), b("BT", 0, n), b("flip", i, i + 1), A.mult)
            n *= 2
        tt(b("tmpe"), b("I"), b("SHD"), A.subtract)
        for n, src, c in (("TRI64", "TRI", 64.0), ("D64", "tmpe", 64.0), ("Dm64", "tmpe", -64.0)):
            act(b(n), b(src), F.Copy, scale=c)
        for i in range(4):
            ts(b("MASKN", 128 * i, 128 * i + 128), b("Qb"), col(0), A.is_le, -64.0, A.mult)
        ms(b("BAND"), 0.0)
        ms(b("BAND", 112, 128), 1.0)

    def consts_c():
        ms(b("ONES"), 1.0)
        ms(b("Y0"), 1.0)
        ms(b("Y0", 128, 256), 65.0)
        ts(b("W8"), b("Qb", 0, 8), 16.0, A.mult, col(2), A.add)
        for h in (0, 8):
            ts(b("DUM", h, h + 8), b("W8"), float(NDUM), A.add)
            ts(b("DD", h, h + 8), b("W8"), float(NDUMP), A.add)
        ts(b("DTOK"), b("W8"), float(TDUMP), A.add)
        ts(col(4), col(2), -1.0, A.mult, 15.0, A.add)
        ts(col(6), col(2), 0.0, A.is_gt)
        ts(b("IDT", 0, 16), b("Qb", 0, 16), col(4), A.is_equal)

    def round_start(r):
        src = b("Qi") if r == 0 else b("QF")
        if r:
            tt(b("HK"), b("LK"), b("HMQ"), A.mult)
            tt(b("QF"), b("HK"), b("LQ"), A.add)
        cp(b("Ql"), src)
        qi = src
        if r:
            xq(0)
            xq(1)
            qi = b("Qi2")
            cp(qi, src)
        ts(b("Q4i"), qi, 4, A.arith_shift_right)
        ts(b("Q4m"), b("Q4i"), col(5), A.mult)
        mm([(b("pm", 0, 128), b("Q4m"), b("BO"), True, True)])
        ts(b("QMi"), qi, 15, A.bitwise_and)
        cp(b("QM"), b("QMi"))
        if r == 0:
            tt(b("DQ"), b("I"), b("SHU"), A.subtract)
        tt(b("mk"), b("pm", 0, 128), b("MSK"), A.mult)
        mm([(b("pm", 128, 136), b("mk"), b("SEL"), True, True)])
        mm([(b("ps", 128, 256), b("B0"), b("QM"), True, True)])
        mm([(b("pw", 0, 128), b("DQ"), b("QM"), True, True)])
        cp(b("vl"), b("pm", 128, 136))
        act(b("VC", 0, 8), b("pm", 128, 136), F.Copy)
        ts(b("OH"), b("ps", 128, 256), col(2), A.is_equal)

    def round_rest(r):
        ts(b("P"), b("pw", 0, 128), 16.0, A.add)
        if r:
            ms(b("KGE"), 1.0)
        else:
            cp(b("QF"), b("Qi"))
            travel("QF", "LQ", "E")
        ts(b("uQ"), b("QF"), -1.0, A.mult, 2047.0, A.add)

    hsrc = lambda r: b("QF" if r else "LQ")

    def hash_a(r):
        cp(b("Q16"), hsrc(r))
        mm([(b("pw", 0, 128), b("SHD"), b("Q16"), True, True)])

    def hash_b(r):
        tt(b("HP"), b("pw", 0, 128), hsrc(r), A.mult)
        ts(b("HI"), b("HP"), 5, A.arith_shift_right, 2047, A.bitwise_and)
        ts(b("HM"), b("HI"), 2046.5, A.is_lt)

    def hash_c(r):
        tt(b("HMQ"), b("HI"), b("HM"), A.mult)
        tt(b("HMQ"), b("HMQ"), hsrc(r), A.subtract)
        ts(b("HMQ"), b("HMQ"), col(6), A.mult)

    def gram_mask(h):
        mm([(b("pg%d" % h), b("I"), b("MASKN"), True, False)])

    def gram(left, lefto, right, masked):
        done = {}
        for y in range(2):
            for h in range(2):
                l = []
                for x in (2 * y, 2 * y + 1):
                    gr = 4 * h + x
                    p0 = 32 * (gr // 2)
                    p1 = p0 + (32 if gr % 2 else 16)
                    l.append((b("pg%d" % h, 128 * x, 128 * x + 128), part(b(lefto if gr % 2 else left), p0, p1), part(b(right), p0, p1),
                              not masked, not masked or x == 3))
                if y:
                    wait("T", "sT", done[h])
                done[h] = mm(l)

    def band(gr):
        return b("BAND", 112 - 16 * gr, 240 - 16 * gr)

    def def_m(r, s):
        if r == 0:
            mm([(b("pg1", 384, 512), b("BO"), b("BUF", 384, 512), True, True)])

    def def_a(r, s):
        cp(b("RW"), b("pm", 384, 400))
        ts(b("RW"), b("RW"), 15, A.bitwise_and)
        cp(b("RL"), b("RW"))
        for h in range(2):
            act(b("OHc", 128 * h, 128 * h + 128), ind("IDT", 16, "RL", 8 * h, 8 * h + 8), F.Copy)

    def def_b(r, s):
        if r == 0:
            n0 = 384 + 256 * r + 128
            tt(b("X5"), b("pg1", 384, 512), b("Cc"), A.mult)
            tt(b("C", n0, n0 + 128), b("C", n0, n0 + 128), b("X5"), A.add)
        tt(b("OHN"), b("OHc"), b("N01", 256 * r, 256 * r + 256), A.mult)

    def def_c(r, s):
        tt(ind("C", 1152, "lc", 8, 16), b("OHN", 0, 128), b("OHN", 128, 256), A.max)

    def unmade_m(r):
        l = []
        for s in range(S_):
            q = "QE%d" % (3 * r + s)
            l += [(b("pg0", 256, 384), b("BO"), b(q, 0, 128), s == 0, False), (b("pg0", 256, 384), b("BOm1"), b(q, 128, 256), False, s == S_ - 1)]
        mm(l)

    def unmade(r):
        n1 = 384 + 256 * r
        cp(b("RI", 0, 128), b("pg0", 256, 384))
        ts(b("RA", 0, 128), b("RI", 0, 128), 15, A.bitwise_and)
        ts(b("X5"), b("RA", 0, 128), 0.5, A.is_gt)
        tt(b("L", n1, n1 + 128), b("L", n1, n1 + 128), b("X5"), A.mult)

    def step_a1():
        tt(b("M1"), ind("C", 1024, "vl"), b("OH"), A.mult)
        mm([(b("pm", 0, 128), b("M1"), b("BO"), True, True)])

    def step_a2():
        tt(b("mk"), b("pm", 0, 128), b("MSK"), A.mult)
        mm([(b("pm", 128, 136), b("mk"), b("SEL"), True, True), (b("pm", 256, 384), b("BO"), b("M1"), True, True)])

    def step_a3(late=False):
        cp(b("cl"), b("pm", 128, 136))
        act(b("VC", 8, 16), b("pm", 128, 136), F.Copy)
        if not late:
            act(b("CB"), ind("BT", 1024, "cl"), F.Copy)

    def step_a4():
        ts(b("El"), ind("L", 1024, "cl"), -1.0, A.mult, 2047.0, A.add)

    def act_1():
        act(b("VB"), ind("BT", 1024, "vl"), F.Copy)
        act(b("VBo"), b("VB"), F.Copy, scale=col(3))
        gram("VB", "VBo", "VB", True)

    def act_2(stand=False):
        act(b("EA", 0, 512), b("pg0"), F.Relu, bias=-15.0)
        ts(b("EA", 512, 1024), b("pg1"), 15.5, A.is_gt)
        if stand:
            gram("VB", "VBo", "CB", False)
        mm([(b("pc", 0, 128), band(x), b("EA", 128 * x, 128 * x + 128), x == 0, x == 7) for x in range(8)])

    last = (RO_ - 1, S_ - 1)

    def stood():
        act(b("CB"), ind("BT", 1024, "cl"), F.Copy)
        gram("VB", "VBo", "CB", False)

    def xq(q):
        act(b("XQ", 512 * q, 512 * q + 512), ind("X", 2064, "Ql", 32 * q, 32 * q + 32), F.Copy)

    def df(q):
        tt(b("DF", 512 * q, 512 * q + 512), ind("X", 2064, "El", 32 * q, 32 * q + 32), b("XQ", 512 * q, 512 * q + 512), A.subtract)

    def ab(q):
        act(b("AB", 512 * q, 512 * q + 512), b("DF", 512 * q, 512 * q + 512), F.Abs)

    def es(h):
        ts(b("ES", 512 * h, 512 * h + 512), b("pg%d" % h), 15.5, A.is_gt)

    def words():
        tt(b("CMV"), b("VC", 8, 16), b("VC", 0, 8), A.subtract)
        tt(b("DMC"), b("DUM", 0, 8), b("VC", 8, 16), A.subtract)
        tt(b("VCD"), b("VC"), b("DD"), A.subtract)

    def step(r, s):
        leafc = (r, s) != last
        first = r == 0 and s == 0
        QE = "QE%d" % (3 * r + s)
        yF, yL, yC = b("py", 0, 128), b("py", 128, 256), b("pm", 256, 384)

        def dist(h):
            mm([(b("pd", 0, 128), b("ImB"), b("NA"), False, False) if h else (b("pd", 0, 128), b("IB"), b("KGE"), True, False)] + [(b("pd", 64 * h, 64 * h + 64), b("CONV", 128 * k, 128 * k + 128), b("AB", 1024 * h + k, 1024 * h + 1024, 16), False,
                   h == 1 and k == 15) for k in range(16)])

        def y_pre():
            mm([(b("py", 0, 256), b("I"), b("Y0", 0, 256), True, False),
                (yF, b("Im128"), b("NA"), False, False), (yL, b("Dm64"), b("KGE"), False, False),
                (yF, b("I64"), b("NN"), False, False), (yL, b("I64"), b("NN"), False, False)])
            mm([(yC, b("I"), b("Y0", 0, 128), True, False), (yC, b("D64"), b("KGE"), False, False), (yC, b("I64"), b("NN"), False, False)])

        if s == 0:
            step_a4()
            round_rest(r)
            xq(2)
            df(0)
            ab(0)
            if first:
                xq(3)
                consts_b()
                for h in range(2):
                    gram_mask(h)
                act_1()
                df(1)
                ab(1)
                df(2)
                act_2()
                stood()
                consts_c()
                ab(2)
                df(3)
                ab(3)
                dist(0)
                act(b("NA"), b("pc", 0, 128), F.Sign)
                es(0)
                es(1)
            else:
                act_2()
                df(1)
                xq(3)
                ab(1)
                stood()
                df(2)
                dist(0)
                ab(2)
                df(3)
                es(0)
                act(b("NA"), b("pc", 0, 128), F.Sign)
                es(1)
                ab(3)
        else:
            xq(0)
            df(0)
            act_2(True)
            xq(1)
            ab(0)
            df(1)
            xq(2)
            ab(1)
            es(0)
            df(2)
            es(1)
            dist(0)
            xq(3)
            act(b("NA"), b("pc", 0, 128), F.Sign)
            ab(2)
            if len(fills) == 4:
                fill(2)
        if (r, s) == last:
            fills.extend([lambda: hash_a(r), lambda: hash_b(r), lambda: hash_c(r)])
        elif s == 0 and r:
            fills.extend([lambda: unmade_m(r - 1), lambda: unmade(r - 1)])
        if len(fills) > 2 or s == 0:
            fill()
        mm([(b("pc", 128, 256), band(x), b("ES", 128 * x, 128 * x + 128), x == 0, x == 7) for x in range(8)])
        ts(b("NN"), b("El"), 2047.0, A.is_equal)
        if leafc:
            tt(b("T1"), b("pm", 256, 384), b("N01", 256 * r + 128, 256 * r + 256), A.subtract)
        y_pre()
        if s:
            df(3)
            ab(3)
        ts(b("STD"), b("pc", 128, 256), 0.5, A.is_gt)
        mm([(yC, b("I64"), b("STD"), False, False)])
        dist(1)
        late = len(fills) > 0
        fill(9)
        if not late:
            for h in range(2):
                gram_mask(h)
        act(b("uE"), ind("L", 1024, "cl"), F.Copy)
        if leafc:
            act(b("CV"), ind("C", 1024, "vl"), F.Copy)
        if r == 0:
            act(b("Cc"), ind("C", 1024, "cl"), F.Copy)
        ST, FS, LF, CU = (b("BUF", 128 * i, 128 * i + 128) for i in range(4))
        ts(ST, b("pd", 0, 128), BIG + 620.5, A.is_gt)
        mm([(yC, b("STRI"), ST, False, True)])
        mm([(yF, b("STRI"), ST, False, False), (yL, b("STRI"), ST, False, True)])
        mm([(b("ps", 0, 128), b("TRI64"), ST, True, False)])
        if late:
            gram_mask(0)
        words()
        tt(CU, yC, ST, A.is_le)
        tt(b(QE, 0, 128), CU, b("uQ"), A.mult)
        mm([(b("pm", 0, 128), b(QE, 0, 128), b("BO"), True, True)])
        tt(FS, yF, ST, A.is_le)
        mm([(b("ps", 0, 128), b("BO64"), FS, False, True)])
        if late:
            gram_mask(1)
        tt(LF, yL, ST, A.is_le)
        tt(b("mkq", 0, 128), b("pm", 0, 128), b("MSK"), A.mult)
        mm([(b("pm", 384, 392), b("mkq", 0, 128), b("SEL"), True, True)])
        mm([(b("pd", 128, 384), b("TRI"), b("BUF", 256, 512), True, True)])
        tt(b(QE, 128, 256), CU, b("uE"), A.mult)
        mm([(b("pm", 128, 256), b(QE, 128, 256), b("BO"), True, True)])
        mm([(b("pw", 0, 32), b("CONV", 128 * m, 128 * m + 128), b("BUF", m, 512, 16), m == 0, m == 15) for m in range(16)])
        if (r, s) != last:
            tt(b("P"), b("ps", 0, 128), b("P"), A.min)
            act(b("KGE"), b("P"), F.Sign)
        if (r, s) == last:
            tt(b("KGE"), b("ps", 0, 128), b("KGE"), A.min)
        ts(b("qel", 0, 8), b("pm", 384, 392), -1.0, A.mult, 2047.0, A.add)
        if (r, s) == last:
            tt(b("HK"), b("KGE"), b("HMQ"), A.mult)
            tt(b("SND"), b("HK"), b("QF"), A.add)
            travel("SND", "LAND1", "1")
        elif s == S_ - 1:
            travel("KGE", "LK", "0")
        if leafc:
            tt(b("T2"), b("T1"), b("OH"), A.mult)
        tt(b("X2"), b("pd", 256, 384), b("uE"), A.mult)
        tt(b("X1"), b("pd", 128, 256), b("uQ"), A.mult)
        act(b("QB"), ind("BT", 2048, "qel", 0, 8), F.Copy)
        act(b("QBo"), b("QB"), F.Copy, scale=col(3))
        act(b("QLF"), b("pm", 384, 392), F.Copy, bias=2047.0, scale=-1.0)
        act(b("XQg"), ind("X", 2064, "qel", 0, 8), F.Copy)
        gram("QB", "QBo", "QB", True)
        if s < S_ - 1:
            mm([(b("ps", 128, 256), b("BO"), b("P"), True, False), (b("ps", 128, 256), b("BOm16"), b("KGE"), False, True)])
        tt(b("mkq", 128, 256), b("pm", 128, 256), b("MSK"), A.mult)
        mm([(b("pm", 392, 400), b("mkq", 128, 256), b("SEL"), True, True)])
        act(b("ED", 0, 512), b("pg0"), F.Relu, bias=-15.0)
        act(b("ED", 512, 1024), b("pg1"), F.Relu, bias=-15.0)
        if s < S_ - 1:
            for h in range(2):
                gram_mask(h)
        tt(b("l1"), b("pw", 16, 32), b("VCD"), A.mult)
        tt(b("l2"), b("l1"), b("DD"), A.add)
        cp(b("lc"), b("l2"))
        if s < S_ - 1:
            ts(b("WF"), b("pw", 0, 16), 0.5, A.is_lt)
            tt(b("w6"), b("pw", 16, 32), b("DUM"), A.mult)
            tt(b("x1"), b("WF", 0, 8), b("DMC"), A.mult)
            tt(b("x2"), b("x1"), b("CMV"), A.add)
            tt(b("x3"), b("WF", 8, 16), b("x2"), A.mult)
            tt(b("x4"), b("x3"), b("VC", 0, 8), A.add)
            tt(b("y1"), b("x4"), b("w6", 0, 8), A.max)
            tt(b("VC", 0, 8), b("y1"), b("w6", 8, 16), A.max)
            cp(b("vl"), b("VC", 0, 8))
        ts(b("qel", 8, 16), b("pm", 392, 400), -1.0, A.mult, 2047.0, A.add)
        act(b("XLg"), ind("X", 2064, "qel", 8, 16), F.Copy)
        n1 = 384 + 256 * r
        mm([(b("pc", 256 + 16 * x, 272 + 16 * x), b("ED", 128 * x, 128 * x + 128), b("ONES", 0, 16), True, True) for x in range(8)])
        if leafc:
            tt(ind("C", 1152, "lc", 0, 8), b("CV"), b("T2"), A.subtract)
        if s < S_ - 1:
            ts(b("OH"), b("ps", 128, 256), col(2), A.is_equal)
            step_a1()
        mm([(b("ps", 128, 256), b("I"), b("XQg"), True, False), (b("ps", 128, 256), b("I"), b("XLg"), False, True)])
        act(b("DS"), b("ps", 128, 256), F.Copy, bias=2.0 ** 23, scale=0.5 - 2.0 ** -12)
        act(b("DH"), b("DS"), F.Copy, bias=-2.0 ** 23)
        if s < S_ - 1:
            step_a2()
        tt(b("X3"), b("pd", 256, 384), b("uQ"), A.mult)
        if s == S_ - 1 and r == 0:
            hash_a(r)
            hash_b(r)
        tt(b("mk2"), b("pc", 256, 384), b("MSK"), A.mult)
        mm([(b("pw", 64, 72), b("mk2"), b("SELB"), True, True)])
        mm([(b("ps", 256, 384), b("I"), b("X3"), True, True), (b("ps", 384, 512), b("I"), b("X1"), True, False),
            (b("ps", 384, 512), b("I32"), b("X2"), False, True)])
        if s < S_ - 1:
            step_a3()
            act_1()
        if s == S_ - 1 and r == 0:
            hash_c(r)
        tt(b("d1"), b("pw", 64, 72), b("QLF"), A.max)
        tt(b("d2"), b("d1"), b("DTOK"), A.min)
        cp(b("didx"), b("d2"))
        cp(ind("X", 2192, "didx"), b("DH"))
        if (r, s) == last:
            cp(b("X", 2047, 2048), b("xsave", 0, 1))
            dma("Y", T.yd[:], T.X[:, 0:2048], r=[b("X", 0, 2048)])
        tt(ind("L", 1152, "lc", 8, 16), b("uE"), b("X2"), A.subtract)
        tt(b("L", n1, n1 + 256), b("ps", 256, 512), b("L", n1, n1 + 256), A.add)
        if s < S_ - 1:
            step_a4()
        if r == 0 or s == 0:
            fills.extend([lambda: def_m(r, s), lambda: def_a(r, s), lambda: def_b(r, s), lambda: def_c(r, s)])
        if s == S_ - 1:
            fill(9)
        if (r, s) == last:
            unmade_m(r)
            unmade(r)

    def travel(src, land, tag):
        sent = [0]
        deps("G", [b(src)], [], "loc" + tag, 0)
        for call in plan(core, T.cores, topo):
            tr = []
            for d, en in call:
                e = (T.rank_of(d) - rank) % 8
                rid, pid = topo.addr(d, core)
                tr.append(RemoteDMATransfer(dst_ids=[DstId(rid=rid, pnc=pid)], dma_engine_mask=sum(1 << x for x in en),
                                            remote_sem=T.sem["arr" + tag], src=T[src][:, 16 * e:16 * e + 16],
                                            dst=T[land][:, 16 * e:16 * e + 16]))
                sent[0] += len(en)
            g.remote_dma_fused(tr, local_sem=T.sem["loc" + tag])
        cp(b(land, 0, 16), b(src, 0, 16))
        n = sum(len(en) for s in T.cores if s != core for call in plan(s, T.cores, topo) for d, en in call if d == core)
        K["acc"].setdefault(land, []).append((16, 128, 1, "R", "arr" + tag, n, True))
        K["acc"].setdefault(src, []).append((0, 128, 0, "R", "loc" + tag, sent[0], True))
        K["final"]["arr" + tag] = n
        K["final"]["loc" + tag] = sent[0]

    for r in range(RO_):
        round_start(r)
        if r == 0:
            cp(b("C", 0, 384), b("Ci"))
        step_a1()
        if r == 0:
            ts(b("L", 0, 384), b("Ei"), -1.0, A.mult, 2047.0, A.add)
            cp(b("lsave", 0, 1), b("L", 0, 1))
            ms(b("L", 0, 1), -1.0)
            ms(b("X", 2048, 2192), 512.0)
            cp(b("xsave", 0, 1), b("X", 2047, 2048))
            ms(b("X", 2047, 2048), 4096.0)
            xq(0)
        step_a2()
        step_a3(True)
        if r == 0:
            xq(1)
        else:
            for h in range(2):
                gram_mask(h)
            act_1()
        for s in range(S_):
            step(r, s)
    act(b("YE", 0, 384), b("L", 0, 384), F.Copy, bias=2047.0, scale=-1.0)
    act(b("YE", 0, 1), b("lsave", 0, 1), F.Copy, bias=2047.0, scale=-1.0)
    for r in range(RO_):
        n1 = 384 + 256 * r
        for j, o in ((128, 0), (0, 1)):
            act(b("YE", n1 + o, n1 + 256, 2), b("L", n1 + j, n1 + j + 128), F.Copy, bias=2047.0, scale=-1.0)
    dma("S", T.ye[:], T.YE[:], r=[b("YE")])
    dma("Y", T.yr[:], T.LAND1[:], r=[b("LAND1")])
    for s, v in K["final"].items():
        K["known"]["G"].pop(s, None)
        wait("G", s, v)
